import numpy as np
import ml_dtypes


def mxq(x, axis, fmt="e4m3"):
    dtype, down = {"e4m3": (ml_dtypes.float8_e4m3fn, 7), "e5m2": (ml_dtypes.float8_e5m2, 14)}[fmt]
    v = np.moveaxis(np.asarray(x, np.float32).astype(ml_dtypes.bfloat16).astype(np.float64), axis, -1)
    blocks = v.reshape(v.shape[:-1] + (-1, 32))
    amax = np.abs(blocks).max(-1, keepdims=True)
    byte = np.maximum(np.where(amax > 0, np.frexp(amax)[1] - 1 + 127, 0) - down, 1)
    scale = np.exp2(byte - 127.0)
    codes = (blocks / scale).astype(np.float32).astype(dtype).astype(np.float64)
    return np.moveaxis((codes * scale).reshape(v.shape), -1, axis)


WIDE = False


def mx_kscale(k):
    if not WIDE:
        return np.ones(k)
    levels = np.array([10, -10, 5, -5, 0])
    if k % 512:
        return np.exp2(np.random.permutation(np.resize(levels, k // 32))).repeat(32)
    a = np.empty((k // 512, 16))
    for p in range(k // 512):
        a[p, :8] = np.random.permutation(np.resize(levels, 8))
        for g in range(8):
            far = levels[np.abs(levels - a[p, g]) >= 10]
            a[p, g + 8] = far[np.random.randint(len(far))]
    return np.exp2(a.ravel()).repeat(32)


def f64(x):
    return np.asarray(x).astype(np.float64)


def striped(idx):
    return np.tile(idx.reshape(-1, 16).T, (8, 1)).astype(np.uint16)


def unstriped(offs):
    return offs[:16].T.reshape(-1).astype(np.int64)


E2M1 = np.array([0.0, 0.5, 1.0, 1.5, 2.0, 3.0, 4.0, 6.0, -0.0, -0.5, -1.0, -1.5, -2.0, -3.0, -4.0, -6.0])


def pack_weight(w, fmt):
    k, n = w.shape
    w = f64(np.asarray(w, np.float32).astype(ml_dtypes.bfloat16)).reshape(k // 32, 32, n)
    amax = np.abs(w).max(1)
    if fmt == "e4m3":
        byte = np.frexp(amax)[1] - 1 + 127 - 7
    else:
        mant, ex = np.frexp(amax / 6.0)
        byte = np.where(mant > 0.5, ex, ex - 1) + 127
    byte = np.clip(np.where(amax > 0, byte, 1), 1, 254)
    scaled = (w * np.exp2(127.0 - byte)[:, None, :]).reshape(k, n).astype(np.float32)
    by_word = np.ascontiguousarray(scaled.reshape(k // 512, 128, 4, n).transpose(0, 1, 3, 2))
    if fmt == "e4m3":
        words = by_word.astype(ml_dtypes.float8_e4m3fn).view(np.uint8)
    else:
        c = by_word.astype(ml_dtypes.float4_e2m1fn).view(np.uint8) & 0xF
        words = (c[..., 0::2] | (c[..., 1::2] << 4)).reshape(k // 512, 128, 2 * n)
    return np.ascontiguousarray(words), np.ascontiguousarray(byte.astype(np.uint8).reshape(k // 512, 16, n))


def unpack_weight(words, scales, fmt):
    g, _, n = scales.shape
    words = np.ascontiguousarray(words).reshape(g, 128, n, -1)
    if fmt == "e4m3":
        vals = words.view(ml_dtypes.float8_e4m3fn).astype(np.float64)
    else:
        nib = np.empty((g, 128, n, 4), np.uint8)
        nib[..., 0::2] = words & 0xF
        nib[..., 1::2] = words >> 4
        vals = E2M1[nib]
    vals = vals * np.repeat(np.exp2(scales.astype(np.float64) - 127.0), 8, axis=1)[..., None]
    return vals.transpose(0, 1, 3, 2).reshape(g * 512, n)


def pack_table(v):
    words, scales = pack_weight(v, "e4m3")
    return np.concatenate([words.reshape(words.shape[0], -1), scales.reshape(scales.shape[0], -1)], axis=1)


def unpack_table(tab):
    g, t = tab.shape[0], tab.shape[1] // 528
    return unpack_weight(tab[:, :512 * t].reshape(g, 128, t, 4), tab[:, 512 * t:].reshape(g, 16, t), "e4m3")


K, L, M, T, S = 512, 1536, 256, 4096, 1024


def setup_inputs():
    n = np.random.standard_normal
    s1 = mx_kscale(K)[:, None]
    s2 = mx_kscale(L)[:, None]
    p_w4 = pack_weight(n((K, M)) / np.sqrt(K) / s1, "e2m1")
    return {
        "tab": pack_table(n((K, T)) * s1),
        "w4_words": p_w4[0],
        "w4_scales": p_w4[1],
        "x": (n((L, S)) * s2).astype(np.float32),
        "u": (n((L, M)) / np.sqrt(L) / s2).astype(np.float32),
        "b": (0.3 * n(256)).astype(np.float32),
        "offs": striped(np.random.permutation(T)[:S]),
    }


def reference(tab, w4_words, w4_scales, x, u, b, offs):
    tab_ = unpack_table(tab)[:, unstriped(offs)]
    w4_ = unpack_weight(w4_words, w4_scales, "e2m1")
    x_ = mxq(f64(x), 0, "e4m3")
    u_ = mxq(f64(u), 0, "e4m3")
    y = tab_.T @ w4_ + x_.T @ u_
    return y + f64(b)[None, :]

@@ -1,0 +1,213 @@
+from contextlib import ExitStack
+
+import concourse.mybir as mybir
+from concourse.masks import make_identity
+
+K, L, M, T, S = 512, 1536, 256, 4096, 1024
+FLOPS = 2 * S * M * (K + L)
+
+F32 = mybir.dt.float32
+BF16 = mybir.dt.bfloat16
+I32 = mybir.dt.int32
+U32 = mybir.dt.uint32
+U16 = mybir.dt.uint16
+U8 = mybir.dt.uint8
+E4M3 = mybir.dt.float8_e4m3fn_x4
+E2M1 = mybir.dt.float4_e2m1fn_x4
+ADD = mybir.AluOpType.add
+
+P = 128
+PACK = 4
+K_PASS = P * PACK
+PASSES = L // K_PASS
+N_TILE = 128
+LAST = 768
+
+
+def tile_list_tabx_tm_bias_kernel(tc, tab, w4_words, w4_scales, x, u, b, offs, out):
+    nc = tc.nc
+    with ExitStack() as ctx:
+        keep = ctx.enter_context(tc.tile_pool(name="keep", bufs=1))
+        psum = ctx.enter_context(tc.psum_pool(name="psum", bufs=8))
+
+        def held(shape, dtype, name):
+            return keep.tile(shape, dtype, name=name, align_bytes=64)
+
+        offsets = keep.tile([P, S // 16], U16, name="offsets")
+        tab_words = held([P, T], I32, "tab_words")
+        tab_scales = held([P, T // 4], I32, "tab_scales")
+        w4_codes = held([P, 2 * M], U8, "w4_codes")
+        w4_plane = held([P, M // 4], I32, "w4_plane")
+        b_col = held([P, 2], F32, "b_col")
+        u_raw = held([P, PASSES, PACK, M], F32, "u_raw")
+        x_raw = held([P, PASSES, PACK, S], F32, "x_raw")
+
+        def load_u(g):
+            rows = u[g * K_PASS : (g + 1) * K_PASS, :]
+            nc.sync.dma_start(u_raw[:, g], rows.rearrange("(p i) n -> p i n", i=PACK))
+
+        def load_x(g, lo, hi):
+            rows = x[g * K_PASS : (g + 1) * K_PASS, :].rearrange("(p i) j -> p i j", i=PACK)
+            nc.sync.dma_start(x_raw[:, g, :, lo:hi], rows[:, :, lo:hi])
+
+        load_u(0)
+        load_u(1)
+        nc.sync.dma_start(offsets[:], offs)
+        nc.sync.dma_start(tab_words[:], tab[0, 0 : 4 * P * T].rearrange("(p w) -> p w", p=P).bitcast(I32))
+        nc.sync.dma_start(b_col[:], b.rearrange("(p c) -> p c", c=2))
+        nc.sync.dma_start(w4_codes[:].bitcast(I32), w4_words[0].bitcast(I32))
+        nc.vector.memset(tab_scales[:], 0)
+        nc.vector.memset(w4_plane[:], 0)
+        nc.vector.memset(x_raw[:, :, 0, 0:S:P], 0.0)
+        nc.vector.memset(u_raw[:, 2, 0, 0:1], 0.0)
+        scale_rows = tab[0, 4 * P * T :].rearrange("(q r t) -> r q t", q=4, r=4)
+        for r in range(4):
+            nc.sync.dma_start(tab_scales[r:P:32, :], scale_rows[r].bitcast(I32))
+        load_x(0, 0, S)
+        w4_scale_rows = w4_scales[0].rearrange("(q r) n -> r q n", r=4)
+        for r in range(4):
+            nc.sync.dma_start(w4_plane[r:P:32, :], w4_scale_rows[r].bitcast(I32))
+        load_u(2)
+        load_x(1, 0, 512)
+        load_x(2, 0, 512)
+        load_x(1, 512, S)
+        load_x(2, 512, LAST)
+        load_x(2, LAST, S)
+
+        def interleave(copy, grouped, raw):
+            copy(grouped.rearrange("p (c i) t -> p c t i", i=4), raw.rearrange("p t (c i) -> p c t i", i=4))
+
+        def quantize(codes, plane, grouped):
+            nc.vector.quantize_mx(out=codes.bitcast(E4M3), scales=plane, in_=grouped.rearrange("p w t -> p (w t)"))
+
+        u_codes = [held([P, M], U32, "u_codes%d" % g) for g in range(PASSES)]
+        u_plane = [held([P, M], U8, "u_plane%d" % g) for g in range(PASSES)]
+        u_grouped = [held([P, M, PACK], BF16, "u_grouped%d" % g) for g in range(PASSES)]
+
+        def quantize_u(g):
+            quantize(u_codes[g][:], u_plane[g][:], u_grouped[g][:])
+
+        x_codes = [held([P, S], U32, "x_codes%d" % g) for g in range(PASSES)]
+        x_plane = [held([P, S], U8, "x_plane%d" % g) for g in range(PASSES)]
+        x_grouped = [held([P, S, PACK], BF16, "x_grouped%d" % g) for g in range(PASSES)]
+
+        def interleave_x(g, lo, hi, vector_tokens):
+            mid = hi - vector_tokens
+            if lo < mid:
+                interleave(nc.scalar.copy, x_grouped[g][:, lo:mid, :], x_raw[:, g, :, lo:mid])
+            if mid < hi:
+                interleave(nc.vector.tensor_copy, x_grouped[g][:, mid:hi, :], x_raw[:, g, :, mid:hi])
+
+        def quantize_x(g, lo, hi):
+            quantize(x_codes[g][:, lo:hi], x_plane[g][:, lo:hi], x_grouped[g][:, lo:hi, :])
+
+        interleave(nc.scalar.copy, u_grouped[0][:], u_raw[:, 0])
+        interleave(nc.scalar.copy, u_grouped[1][:], u_raw[:, 1])
+        quantize_u(0)
+        quantize_u(1)
+
+        ident = held([P, P], F32, "ident")
+        make_identity(nc, ident[:])
+        bias_bank = psum.tile([P, 2, P], F32, name="bank")
+        for c in range(2):
+            nc.tensor.transpose(bias_bank[:, c, :], b_col[:, c : c + 1].to_broadcast([P, P]), ident[:])
+        bias = held([P, M], F32, "bias")
+        nc.vector.tensor_copy(bias[:].rearrange("p (n c) -> p n c", c=2), bias_bank[:].rearrange("p c n -> p n c"))
+
+        got_words = held([P, S], U32, "got_words")
+        got_scales = held([P, S], U8, "got_scales")
+        for lo in range(0, S, 512):
+            picks = offsets[:, lo // 16 : (lo + 512) // 16]
+            nc.vector.tensor_copy(got_words[:, lo : lo + 512], tab_words[:].bitcast(U32).indirect(picks))
+            nc.vector.tensor_copy(got_scales[:, lo : lo + 512], tab_scales[:].bitcast(U8).indirect(picks))
+
+        acc = {}
+
+        def table_pass(t, h):
+            acc[t, h] = psum.tile([P, N_TILE], F32, name="bank")
+            tok = slice(t * P, (t + 1) * P)
+            nc.tensor.matmul_mx(
+                out=acc[t, h][:],
+                lhsT=got_words[:, tok].bitcast(E4M3),
+                lhsT_scale=got_scales[:, tok],
+                rhs=w4_codes[:, 2 * N_TILE * h : 2 * N_TILE * (h + 1)].bitcast(E2M1),
+                rhs_scale=w4_plane[:].bitcast(U8)[:, N_TILE * h : N_TILE * (h + 1)],
+                start=True,
+                stop=False,
+            )
+
+        def x_pass(g, t, h):
+            tok = slice(t * P, (t + 1) * P)
+            col = slice(h * N_TILE, (h + 1) * N_TILE)
+            nc.tensor.matmul_mx(
+                out=acc[t, h][:],
+                lhsT=x_codes[g][:, tok].bitcast(E4M3),
+                lhsT_scale=x_plane[g][:, tok],
+                rhs=u_codes[g][:, col].bitcast(E4M3),
+                rhs_scale=u_plane[g][:, col],
+                start=False,
+                stop=(g == PASSES - 1),
+            )
+
+        def table_passes(tiles):
+            for t in tiles:
+                for h in range(2):
+                    table_pass(t, h)
+
+        def x_passes(g, tiles):
+            for t in tiles:
+                for h in range(2):
+                    x_pass(g, t, h)
+
+        result = held([P, S // P, M], F32, "result")
+        out_tiles = out.rearrange("(t p) n -> p t n", p=P)
+
+        def add_bias(tiles):
+            for t in tiles:
+                for h in range(2):
+                    col = slice(h * N_TILE, (h + 1) * N_TILE)
+                    nc.vector.tensor_tensor(result[:, t, col], acc[t, h][:], bias[:, col], ADD)
+
+        def store(lo, hi):
+            nc.sync.dma_start(out_tiles[:, lo:hi, :], result[:, lo:hi, :])
+
+        early, late = range(0, 4), range(4, 8)
+
+        table_passes(early)
+        for lo in range(0, S, 256):
+            interleave_x(0, lo, lo + 256, 64)
+            quantize_x(0, lo, lo + 256)
+        x_passes(0, early)
+        interleave(nc.scalar.copy, u_grouped[2][:], u_raw[:, 2])
+        quantize_u(2)
+        for lo in range(0, 512, 256):
+            interleave_x(1, lo, lo + 256, 80)
+            quantize_x(1, lo, lo + 256)
+        x_passes(1, early)
+        for lo in range(0, 512, 256):
+            interleave_x(2, lo, lo + 256, 96)
+            quantize_x(2, lo, lo + 256)
+            x_passes(2, range(lo // P, lo // P + 2))
+        for lo in range(512, S, 256):
+            interleave_x(1, lo, lo + 256, 64)
+        add_bias((0, 1))
+        store(0, 2)
+        add_bias((2, 3))
+        store(2, 4)
+        for lo in range(512, S, 256):
+            quantize_x(1, lo, lo + 256)
+        table_passes(late)
+        x_passes(0, late)
+        x_passes(1, late)
+        interleave_x(2, 512, LAST, 96)
+        quantize_x(2, 512, LAST)
+        x_passes(2, (4, 5))
+        interleave_x(2, LAST, S, 96)
+        quantize_x(2, LAST, S)
+        x_passes(2, (6, 7))
+        add_bias((4, 5))
+        store(4, 6)
+        add_bias((6,))
+        store(6, 7)
+        add_bias((7,))
+        store(7, 8)

@@ -20,8 +20,7 @@ P = 128
 PACK = 4
 K_PASS = P * PACK
 PASSES = L // K_PASS
-N_TILE = 128
-LAST = 768
+HALF = M // 2
 
 
 def tile_list_tabx_tm_bias_kernel(tc, tab, w4_words, w4_scales, x, u, b, offs, out):
@@ -39,40 +38,38 @@ def tile_list_tabx_tm_bias_kernel(tc, tab, w4_words, w4_scales, x, u, b, offs, o
         w4_codes = held([P, 2 * M], U8, "w4_codes")
         w4_plane = held([P, M // 4], I32, "w4_plane")
         b_col = held([P, 2], F32, "b_col")
-        u_raw = held([P, PASSES, PACK, M], F32, "u_raw")
-        x_raw = held([P, PASSES, PACK, S], F32, "x_raw")
+        u_raw = {}
+        x_raw = {}
 
-        def load_u(g):
-            rows = u[g * K_PASS : (g + 1) * K_PASS, :]
-            nc.sync.dma_start(u_raw[:, g], rows.rearrange("(p i) n -> p i n", i=PACK))
+        def load_u(lo, hi):
+            raw = held([P, hi - lo, PACK * M], F32, "u_raw%d" % lo)
+            rows = u[lo * K_PASS : hi * K_PASS, :].rearrange("(g p i) n -> p g (i n)", p=P, i=PACK)
+            nc.sync.dma_start(raw[:], rows)
+            for g in range(lo, hi):
+                u_raw[g] = raw[:, g - lo, :].rearrange("p (i n) -> p i n", i=PACK)
 
         def load_x(g, lo, hi):
+            raw = held([P, PACK, hi - lo], F32, "x_raw%d_%d" % (g, lo))
             rows = x[g * K_PASS : (g + 1) * K_PASS, :].rearrange("(p i) j -> p i j", i=PACK)
-            nc.sync.dma_start(x_raw[:, g, :, lo:hi], rows[:, :, lo:hi])
+            nc.sync.dma_start(raw[:], rows[:, :, lo:hi])
+            x_raw[g, lo] = raw
 
-        load_u(0)
-        load_u(1)
-        nc.sync.dma_start(offsets[:], offs)
-        nc.sync.dma_start(tab_words[:], tab[0, 0 : 4 * P * T].rearrange("(p w) -> p w", p=P).bitcast(I32))
-        nc.sync.dma_start(b_col[:], b.rearrange("(p c) -> p c", c=2))
-        nc.sync.dma_start(w4_codes[:].bitcast(I32), w4_words[0].bitcast(I32))
-        nc.vector.memset(tab_scales[:], 0)
-        nc.vector.memset(w4_plane[:], 0)
-        nc.vector.memset(x_raw[:, :, 0, 0:S:P], 0.0)
-        nc.vector.memset(u_raw[:, 2, 0, 0:1], 0.0)
-        scale_rows = tab[0, 4 * P * T :].rearrange("(q r t) -> r q t", q=4, r=4)
-        for r in range(4):
-            nc.sync.dma_start(tab_scales[r:P:32, :], scale_rows[r].bitcast(I32))
-        load_x(0, 0, S)
-        w4_scale_rows = w4_scales[0].rearrange("(q r) n -> r q n", r=4)
-        for r in range(4):
-            nc.sync.dma_start(w4_plane[r:P:32, :], w4_scale_rows[r].bitcast(I32))
-        load_u(2)
-        load_x(1, 0, 512)
-        load_x(2, 0, 512)
-        load_x(1, 512, S)
-        load_x(2, 512, LAST)
-        load_x(2, LAST, S)
+        def load_small():
+            nc.sync.dma_start(b_col[:], b.rearrange("(p c) -> p c", c=2))
+            nc.sync.dma_start(w4_codes[:].bitcast(I32), w4_words[0].bitcast(I32))
+
+        def load_words():
+            nc.sync.dma_start(tab_words[:], tab[0, 0 : 4 * P * T].rearrange("(p w) -> p w", p=P).bitcast(I32))
+
+        def load_tab_scales():
+            scale_rows = tab[0, 4 * P * T :].rearrange("(q r t) -> r q t", q=4, r=4)
+            for r in range(4):
+                nc.sync.dma_start(tab_scales[r:P:32, :], scale_rows[r].bitcast(I32))
+
+        def load_w4_scales(rows):
+            w4_scale_rows = w4_scales[0].rearrange("(q r) n -> r q n", r=4)
+            for r in rows:
+                nc.sync.dma_start(w4_plane[r:P:32, :], w4_scale_rows[r].bitcast(I32))
 
         def interleave(copy, grouped, raw):
             copy(grouped.rearrange("p (c i) t -> p c t i", i=4), raw.rearrange("p t (c i) -> p c t i", i=4))
@@ -84,6 +81,13 @@ def tile_list_tabx_tm_bias_kernel(tc, tab, w4_words, w4_scales, x, u, b, offs, o
         u_plane = [held([P, M], U8, "u_plane%d" % g) for g in range(PASSES)]
         u_grouped = [held([P, M, PACK], BF16, "u_grouped%d" % g) for g in range(PASSES)]
 
+        def interleave_u(g, on_vector=0):
+            mid = M - on_vector
+            if mid > 0:
+                interleave(nc.scalar.copy, u_grouped[g][:, 0:mid, :], u_raw[g][:, :, 0:mid])
+            if mid < M:
+                interleave(nc.vector.tensor_copy, u_grouped[g][:, mid:M, :], u_raw[g][:, :, mid:M])
+
         def quantize_u(g):
             quantize(u_codes[g][:], u_plane[g][:], u_grouped[g][:])
 
@@ -91,123 +95,127 @@ def tile_list_tabx_tm_bias_kernel(tc, tab, w4_words, w4_scales, x, u, b, offs, o
         x_plane = [held([P, S], U8, "x_plane%d" % g) for g in range(PASSES)]
         x_grouped = [held([P, S, PACK], BF16, "x_grouped%d" % g) for g in range(PASSES)]
 
-        def interleave_x(g, lo, hi, vector_tokens):
-            mid = hi - vector_tokens
+        def interleave_x(g, base, lo, hi, on_vector):
+            raw = x_raw[g, base]
+            mid = hi - on_vector
             if lo < mid:
-                interleave(nc.scalar.copy, x_grouped[g][:, lo:mid, :], x_raw[:, g, :, lo:mid])
+                interleave(nc.scalar.copy, x_grouped[g][:, lo:mid, :], raw[:, :, lo - base : mid - base])
             if mid < hi:
-                interleave(nc.vector.tensor_copy, x_grouped[g][:, mid:hi, :], x_raw[:, g, :, mid:hi])
+                interleave(nc.vector.tensor_copy, x_grouped[g][:, mid:hi, :], raw[:, :, mid - base : hi - base])
 
         def quantize_x(g, lo, hi):
             quantize(x_codes[g][:, lo:hi], x_plane[g][:, lo:hi], x_grouped[g][:, lo:hi, :])
 
-        interleave(nc.scalar.copy, u_grouped[0][:], u_raw[:, 0])
-        interleave(nc.scalar.copy, u_grouped[1][:], u_raw[:, 1])
-        quantize_u(0)
-        quantize_u(1)
-
-        ident = held([P, P], F32, "ident")
-        make_identity(nc, ident[:])
-        bias_bank = psum.tile([P, 2, P], F32, name="bank")
-        for c in range(2):
-            nc.tensor.transpose(bias_bank[:, c, :], b_col[:, c : c + 1].to_broadcast([P, P]), ident[:])
         bias = held([P, M], F32, "bias")
-        nc.vector.tensor_copy(bias[:].rearrange("p (n c) -> p n c", c=2), bias_bank[:].rearrange("p c n -> p n c"))
+
+        def spread_bias():
+            ident = held([P, P], F32, "ident")
+            make_identity(nc, ident[:])
+            bias_bank = psum.tile([P, 2, P], F32, name="bank")
+            for c in range(2):
+                nc.tensor.transpose(bias_bank[:, c, :], b_col[:, c : c + 1].to_broadcast([P, P]), ident[:])
+            nc.vector.tensor_copy(bias[:].rearrange("p (n c) -> p n c", c=2), bias_bank[:].rearrange("p c n -> p n c"))
 
         got_words = held([P, S], U32, "got_words")
         got_scales = held([P, S], U8, "got_scales")
-        for lo in range(0, S, 512):
-            picks = offsets[:, lo // 16 : (lo + 512) // 16]
-            nc.vector.tensor_copy(got_words[:, lo : lo + 512], tab_words[:].bitcast(U32).indirect(picks))
-            nc.vector.tensor_copy(got_scales[:, lo : lo + 512], tab_scales[:].bitcast(U8).indirect(picks))
+
+        def gather_words(lo, hi):
+            picks = offsets[:, lo // 16 : hi // 16]
+            nc.vector.tensor_copy(got_words[:, lo:hi], tab_words[:].bitcast(U32).indirect(picks))
+
+        def gather_scales(lo, hi):
+            picks = offsets[:, lo // 16 : hi // 16]
+            nc.vector.tensor_copy(got_scales[:, lo:hi], tab_scales[:].bitcast(U8).indirect(picks))
 
         acc = {}
 
-        def table_pass(t, h):
-            acc[t, h] = psum.tile([P, N_TILE], F32, name="bank")
-            tok = slice(t * P, (t + 1) * P)
-            nc.tensor.matmul_mx(
-                out=acc[t, h][:],
-                lhsT=got_words[:, tok].bitcast(E4M3),
-                lhsT_scale=got_scales[:, tok],
-                rhs=w4_codes[:, 2 * N_TILE * h : 2 * N_TILE * (h + 1)].bitcast(E2M1),
-                rhs_scale=w4_plane[:].bitcast(U8)[:, N_TILE * h : N_TILE * (h + 1)],
-                start=True,
-                stop=False,
-            )
-
-        def x_pass(g, t, h):
-            tok = slice(t * P, (t + 1) * P)
-            col = slice(h * N_TILE, (h + 1) * N_TILE)
-            nc.tensor.matmul_mx(
-                out=acc[t, h][:],
-                lhsT=x_codes[g][:, tok].bitcast(E4M3),
-                lhsT_scale=x_plane[g][:, tok],
-                rhs=u_codes[g][:, col].bitcast(E4M3),
-                rhs_scale=u_plane[g][:, col],
-                start=False,
-                stop=(g == PASSES - 1),
-            )
-
         def table_passes(tiles):
             for t in tiles:
+                tok = slice(t * P, (t + 1) * P)
                 for h in range(2):
-                    table_pass(t, h)
+                    nc.tensor.matmul_mx(
+                        out=acc[t][:, HALF * h : HALF * (h + 1)],
+                        lhsT=got_words[:, tok].bitcast(E4M3),
+                        lhsT_scale=got_scales[:, tok],
+                        rhs=w4_codes[:, 2 * HALF * h : 2 * HALF * (h + 1)].bitcast(E2M1),
+                        rhs_scale=w4_plane[:].bitcast(U8)[:, HALF * h : HALF * (h + 1)],
+                        start=False,
+                        stop=False,
+                    )
 
         def x_passes(g, tiles):
             for t in tiles:
-                for h in range(2):
-                    x_pass(g, t, h)
+                if g == 0:
+                    acc[t] = psum.tile([P, M], F32, name="bank")
+                tok = slice(t * P, (t + 1) * P)
+                nc.tensor.matmul_mx(
+                    out=acc[t][:],
+                    lhsT=x_codes[g][:, tok].bitcast(E4M3),
+                    lhsT_scale=x_plane[g][:, tok],
+                    rhs=u_codes[g][:].bitcast(E4M3),
+                    rhs_scale=u_plane[g][:],
+                    start=(g == 0),
+                    stop=(g == PASSES - 1),
+                )
 
         result = held([P, S // P, M], F32, "result")
         out_tiles = out.rearrange("(t p) n -> p t n", p=P)
 
         def add_bias(tiles):
             for t in tiles:
-                for h in range(2):
-                    col = slice(h * N_TILE, (h + 1) * N_TILE)
-                    nc.vector.tensor_tensor(result[:, t, col], acc[t, h][:], bias[:, col], ADD)
+                nc.vector.tensor_tensor(result[:, t, :], acc[t][:], bias[:], ADD)
 
         def store(lo, hi):
             nc.sync.dma_start(out_tiles[:, lo:hi, :], result[:, lo:hi, :])
 
-        early, late = range(0, 4), range(4, 8)
+        nc.vector.memset(tab_scales[:], 0)
+        nc.vector.memset(w4_plane[:], 0)
+        load_words()
+        load_tab_scales()
+        nc.sync.dma_start(offsets[:], offs)
+        load_u(0, 3)
+        load_x(0, 0, 512)
+        load_small()
+        load_x(1, 0, 512)
+        load_w4_scales((0, 1))
+        load_x(2, 0, 512)
+        load_w4_scales((2, 3))
+        load_x(0, 512, S)
+        load_x(1, 512, S)
+        load_x(2, 512, 768)
+        load_x(2, 768, 896)
+        load_x(2, 896, S)
 
-        table_passes(early)
-        for lo in range(0, S, 256):
-            interleave_x(0, lo, lo + 256, 64)
-            quantize_x(0, lo, lo + 256)
-        x_passes(0, early)
-        interleave(nc.scalar.copy, u_grouped[2][:], u_raw[:, 2])
-        quantize_u(2)
-        for lo in range(0, 512, 256):
-            interleave_x(1, lo, lo + 256, 80)
-            quantize_x(1, lo, lo + 256)
-        x_passes(1, early)
-        for lo in range(0, 512, 256):
-            interleave_x(2, lo, lo + 256, 96)
-            quantize_x(2, lo, lo + 256)
-            x_passes(2, range(lo // P, lo // P + 2))
-        for lo in range(512, S, 256):
-            interleave_x(1, lo, lo + 256, 64)
-        add_bias((0, 1))
-        store(0, 2)
-        add_bias((2, 3))
-        store(2, 4)
-        for lo in range(512, S, 256):
-            quantize_x(1, lo, lo + 256)
-        table_passes(late)
-        x_passes(0, late)
-        x_passes(1, late)
-        interleave_x(2, 512, LAST, 96)
-        quantize_x(2, 512, LAST)
-        x_passes(2, (4, 5))
-        interleave_x(2, LAST, S, 96)
-        quantize_x(2, LAST, S)
-        x_passes(2, (6, 7))
+        for lo in range(0, S, 512):
+            gather_words(lo, lo + 512)
+            gather_scales(lo, lo + 512)
+        for g in range(PASSES):
+            interleave_u(g, 64)
+            quantize_u(g)
+        spread_bias()
+
+        def unit(g, base, lo, hi, on_vector):
+            interleave_x(g, base, lo, hi, on_vector)
+            quantize_x(g, lo, hi)
+            x_passes(g, range(lo // P, hi // P))
+
+        for g in range(PASSES):
+            for lo in range(0, 512, 256):
+                unit(g, 0, lo, lo + 256, 128)
+            if g == 0:
+                table_passes(range(4))
+        add_bias(range(4))
+        store(0, 4)
+        for g in range(2):
+            for lo in range(512, S, 256):
+                unit(g, 512, lo, lo + 256, 128)
+            if g == 0:
+                table_passes(range(4, 8))
+        unit(2, 512, 512, 768, 128)
+        unit(2, 768, 768, 896, 48)
         add_bias((4, 5))
         store(4, 6)
+        unit(2, 896, 896, S, 64)
         add_bias((6,))
-        store(6, 7)
         add_bias((7,))
-        store(7, 8)
+        store(6, 8)

@@ -36,22 +36,22 @@ def tile_list_tabx_tm_bias_kernel(tc, tab, w4_words, w4_scales, x, u, b, offs, o
         tab_words = held([P, T], I32, "tab_words")
         tab_scales = held([P, T // 4], I32, "tab_scales")
         w4_codes = held([P, 2 * M], U8, "w4_codes")
-        w4_plane = held([P, M // 4], I32, "w4_plane")
         b_col = held([P, 2], F32, "b_col")
         u_raw = {}
         x_raw = {}
 
-        def load_u(lo, hi):
-            raw = held([P, hi - lo, PACK * M], F32, "u_raw%d" % lo)
-            rows = u[lo * K_PASS : hi * K_PASS, :].rearrange("(g p i) n -> p g (i n)", p=P, i=PACK)
-            nc.sync.dma_start(raw[:], rows)
-            for g in range(lo, hi):
-                u_raw[g] = raw[:, g - lo, :].rearrange("p (i n) -> p i n", i=PACK)
+        stage = [held([P, 4 * S], F32, "stage%d" % n) for n in range(3)]
 
-        def load_x(g, lo, hi):
-            raw = held([P, PACK, hi - lo], F32, "x_raw%d_%d" % (g, lo))
+        def load_u(room):
+            rows = u.rearrange("(g p i) n -> p g (i n)", p=P, i=PACK)
+            nc.sync.dma_start(room.rearrange("p (g w) -> p g w", g=PASSES), rows)
+            for g in range(PASSES):
+                u_raw[g] = room[:, g * PACK * M : (g + 1) * PACK * M].rearrange("p (i n) -> p i n", i=PACK)
+
+        def load_x(g, lo, hi, room):
+            raw = room.rearrange("p (i j) -> p i j", i=PACK)
             rows = x[g * K_PASS : (g + 1) * K_PASS, :].rearrange("(p i) j -> p i j", i=PACK)
-            nc.sync.dma_start(raw[:], rows[:, :, lo:hi])
+            nc.sync.dma_start(raw, rows[:, :, lo:hi])
             x_raw[g, lo] = raw
 
         def load_small():
@@ -61,15 +61,17 @@ def tile_list_tabx_tm_bias_kernel(tc, tab, w4_words, w4_scales, x, u, b, offs, o
         def load_words():
             nc.sync.dma_start(tab_words[:], tab[0, 0 : 4 * P * T].rearrange("(p w) -> p w", p=P).bitcast(I32))
 
-        def load_tab_scales():
-            scale_rows = tab[0, 4 * P * T :].rearrange("(q r t) -> r q t", q=4, r=4)
-            for r in range(4):
-                nc.sync.dma_start(tab_scales[r:P:32, :], scale_rows[r].bitcast(I32))
+        staged = held([P, (S + M) // 4], I32, "staged")
+        planes = held([P, (S + M) // 4], I32, "planes")
 
-        def load_w4_scales(rows):
-            w4_scale_rows = w4_scales[0].rearrange("(q r) n -> r q n", r=4)
-            for r in rows:
-                nc.sync.dma_start(w4_plane[r:P:32, :], w4_scale_rows[r].bitcast(I32))
+        def load_scales():
+            nc.sync.dma_start(tab_scales[4:P:8, :], tab[0, 4 * P * T :].rearrange("(q t) -> q t", q=16).bitcast(I32))
+            nc.sync.dma_start(staged[4:P:8, S // 4 :], w4_scales[0].bitcast(I32))
+
+        def move_scales():
+            nc.vector.tensor_copy(staged[:, 0 : S // 4], got_scales[:].bitcast(I32))
+            for r in range(4):
+                nc.sync.dma_start(planes[r:P:32, :], staged[8 * r + 4 : P : 32, :])
 
         def interleave(copy, grouped, raw):
             copy(grouped.rearrange("p (c i) t -> p c t i", i=4), raw.rearrange("p t (c i) -> p c t i", i=4))
@@ -136,9 +138,9 @@ def tile_list_tabx_tm_bias_kernel(tc, tab, w4_words, w4_scales, x, u, b, offs, o
                     nc.tensor.matmul_mx(
                         out=acc[t][:, HALF * h : HALF * (h + 1)],
                         lhsT=got_words[:, tok].bitcast(E4M3),
-                        lhsT_scale=got_scales[:, tok],
+                        lhsT_scale=planes[:].bitcast(U8)[:, tok],
                         rhs=w4_codes[:, 2 * HALF * h : 2 * HALF * (h + 1)].bitcast(E2M1),
-                        rhs_scale=w4_plane[:].bitcast(U8)[:, HALF * h : HALF * (h + 1)],
+                        rhs_scale=planes[:].bitcast(U8)[:, S + HALF * h : S + HALF * (h + 1)],
                         start=False,
                         stop=False,
                     )
@@ -169,29 +171,26 @@ def tile_list_tabx_tm_bias_kernel(tc, tab, w4_words, w4_scales, x, u, b, offs, o
             nc.sync.dma_start(out_tiles[:, lo:hi, :], result[:, lo:hi, :])
 
         nc.vector.memset(tab_scales[:], 0)
-        nc.vector.memset(w4_plane[:], 0)
-        load_words()
-        load_tab_scales()
+        nc.vector.memset(planes[:], 0)
         nc.sync.dma_start(offsets[:], offs)
-        load_u(0, 3)
-        load_x(0, 0, 512)
+        load_words()
         load_small()
-        load_x(1, 0, 512)
-        load_w4_scales((0, 1))
-        load_x(2, 0, 512)
-        load_w4_scales((2, 3))
-        load_x(0, 512, S)
-        load_x(1, 512, S)
-        load_x(2, 512, 768)
-        load_x(2, 768, 896)
-        load_x(2, 896, S)
+        load_scales()
+        load_u(stage[0][:, 0:3072])
+        load_x(0, 0, 512, stage[1][:, 0:2048])
+        load_x(1, 0, 512, stage[1][:, 2048:4096])
+        load_x(2, 0, 512, stage[2][:, 0:2048])
 
         for lo in range(0, S, 512):
-            gather_words(lo, lo + 512)
             gather_scales(lo, lo + 512)
+        move_scales()
+        for lo in range(0, S, 512):
+            gather_words(lo, lo + 512)
         for g in range(PASSES):
-            interleave_u(g, 64)
+            interleave_u(g, 128 if g == 2 else 0)
             quantize_u(g)
+        load_x(0, 512, S, stage[0][:, 0:2048])
+        load_x(1, 512, S, stage[0][:, 2048:4096])
         spread_bias()
 
         def unit(g, base, lo, hi, on_vector):
@@ -200,10 +199,14 @@ def tile_list_tabx_tm_bias_kernel(tc, tab, w4_words, w4_scales, x, u, b, offs, o
             x_passes(g, range(lo // P, hi // P))
 
         for g in range(PASSES):
+            if g == 2:
+                table_passes(range(4))
             for lo in range(0, 512, 256):
                 unit(g, 0, lo, lo + 256, 128)
             if g == 0:
-                table_passes(range(4))
+                load_x(2, 512, 768, stage[1][:, 0:1024])
+                load_x(2, 768, 896, stage[1][:, 1024:1536])
+                load_x(2, 896, S, stage[1][:, 1536:2048])
         add_bias(range(4))
         store(0, 4)
         for g in range(2):

@@ -74,7 +74,7 @@ def tile_list_tabx_tm_bias_kernel(tc, tab, w4_words, w4_scales, x, u, b, offs, o
                 nc.sync.dma_start(planes[r:P:32, :], staged[8 * r + 4 : P : 32, :])
 
         def interleave(copy, grouped, raw):
-            copy(grouped.rearrange("p (c i) t -> p c t i", i=4), raw.rearrange("p t (c i) -> p c t i", i=4))
+            copy(grouped.rearrange("p (c i) t -> p c t i", i=2), raw.rearrange("p t (c i) -> p c t i", i=2))
 
         def quantize(codes, plane, grouped):
             nc.vector.quantize_mx(out=codes.bitcast(E4M3), scales=plane, in_=grouped.rearrange("p w t -> p (w t)"))
@@ -172,8 +172,8 @@ def tile_list_tabx_tm_bias_kernel(tc, tab, w4_words, w4_scales, x, u, b, offs, o
 
         nc.vector.memset(tab_scales[:], 0)
         nc.vector.memset(planes[:], 0)
-        nc.sync.dma_start(offsets[:], offs)
         load_words()
+        nc.sync.dma_start(offsets[:], offs)
         load_small()
         load_scales()
         load_u(stage[0][:, 0:3072])
@@ -220,5 +220,6 @@ def tile_list_tabx_tm_bias_kernel(tc, tab, w4_words, w4_scales, x, u, b, offs, o
         store(4, 6)
         unit(2, 896, 896, S, 64)
         add_bias((6,))
+        store(6, 7)
         add_bias((7,))
-        store(6, 8)
+        store(7, 8)

@@ -37,6 +37,7 @@ def tile_list_tabx_tm_bias_kernel(tc, tab, w4_words, w4_scales, x, u, b, offs, o
         tab_scales = held([P, T // 4], I32, "tab_scales")
         w4_codes = held([P, 2 * M], U8, "w4_codes")
         b_col = held([P, 2], F32, "b_col")
+        b_rows = held([P, P], F32, "b_rows")
         u_raw = {}
         x_raw = {}
 
@@ -55,7 +56,7 @@ def tile_list_tabx_tm_bias_kernel(tc, tab, w4_words, w4_scales, x, u, b, offs, o
             x_raw[g, lo] = raw
 
         def load_small():
-            nc.sync.dma_start(b_col[:], b.rearrange("(p c) -> p c", c=2))
+            nc.sync.dma_start(b_rows[0:2, :], b.rearrange("(c n) -> c n", c=2))
             nc.sync.dma_start(w4_codes[:].bitcast(I32), w4_words[0].bitcast(I32))
 
         def load_words():
@@ -113,10 +114,13 @@ def tile_list_tabx_tm_bias_kernel(tc, tab, w4_words, w4_scales, x, u, b, offs, o
         def spread_bias():
             ident = held([P, P], F32, "ident")
             make_identity(nc, ident[:])
+            turned = psum.tile([P, P], F32, name="bank")
+            nc.tensor.transpose(turned[:], b_rows[:], ident[:])
+            nc.scalar.copy(b_col[:], turned[:, 0:2])
             bias_bank = psum.tile([P, 2, P], F32, name="bank")
             for c in range(2):
                 nc.tensor.transpose(bias_bank[:, c, :], b_col[:, c : c + 1].to_broadcast([P, P]), ident[:])
-            nc.vector.tensor_copy(bias[:].rearrange("p (n c) -> p n c", c=2), bias_bank[:].rearrange("p c n -> p n c"))
+            nc.scalar.copy(bias[:], bias_bank[:].rearrange("p c n -> p (c n)"))
 
         got_words = held([P, S], U32, "got_words")
         got_scales = held([P, S], U8, "got_scales")
@@ -170,13 +174,15 @@ def tile_list_tabx_tm_bias_kernel(tc, tab, w4_words, w4_scales, x, u, b, offs, o
         def store(lo, hi):
             nc.sync.dma_start(out_tiles[:, lo:hi, :], result[:, lo:hi, :])
 
-        nc.vector.memset(tab_scales[:], 0)
+        nc.gpsimd.memset(b_rows[:], 0.0)
+        nc.gpsimd.memset(tab_scales[:, 0:768], 0)
+        nc.vector.memset(tab_scales[:, 768:1024], 0)
         nc.vector.memset(planes[:], 0)
-        load_words()
+        load_u(stage[0][:, 512:3584])
         nc.sync.dma_start(offsets[:], offs)
-        load_small()
         load_scales()
-        load_u(stage[0][:, 0:3072])
+        load_small()
+        load_words()
         load_x(0, 0, 512, stage[1][:, 0:2048])
         load_x(1, 0, 512, stage[1][:, 2048:4096])
         load_x(2, 0, 512, stage[2][:, 0:2048])
@@ -184,11 +190,11 @@ def tile_list_tabx_tm_bias_kernel(tc, tab, w4_words, w4_scales, x, u, b, offs, o
         for lo in range(0, S, 512):
             gather_scales(lo, lo + 512)
         move_scales()
+        for g in range(PASSES):
+            interleave_u(g, 0)
+            quantize_u(g)
         for lo in range(0, S, 512):
             gather_words(lo, lo + 512)
-        for g in range(PASSES):
-            interleave_u(g, 128 if g == 2 else 0)
-            quantize_u(g)
         load_x(0, 512, S, stage[0][:, 0:2048])
         load_x(1, 512, S, stage[0][:, 2048:4096])
         spread_bias()

@@ -75,7 +75,7 @@ def tile_list_tabx_tm_bias_kernel(tc, tab, w4_words, w4_scales, x, u, b, offs, o
                 nc.sync.dma_start(planes[r:P:32, :], staged[8 * r + 4 : P : 32, :])
 
         def interleave(copy, grouped, raw):
-            copy(grouped.rearrange("p (c i) t -> p c t i", i=2), raw.rearrange("p t (c i) -> p c t i", i=2))
+            copy(grouped.rearrange("p (c i) t -> p c t i", i=4), raw.rearrange("p t (c i) -> p c t i", i=4))
 
         def quantize(codes, plane, grouped):
             nc.vector.quantize_mx(out=codes.bitcast(E4M3), scales=plane, in_=grouped.rearrange("p w t -> p (w t)"))
@@ -213,13 +213,14 @@ def tile_list_tabx_tm_bias_kernel(tc, tab, w4_words, w4_scales, x, u, b, offs, o
                 load_x(2, 512, 768, stage[1][:, 0:1024])
                 load_x(2, 768, 896, stage[1][:, 1024:1536])
                 load_x(2, 896, S, stage[1][:, 1536:2048])
-        add_bias(range(4))
+        add_bias((0, 1))
+        unit(0, 512, 512, 768, 64)
+        add_bias((2, 3))
         store(0, 4)
-        for g in range(2):
-            for lo in range(512, S, 256):
-                unit(g, 512, lo, lo + 256, 128)
-            if g == 0:
-                table_passes(range(4, 8))
+        unit(0, 512, 768, S, 64)
+        table_passes(range(4, 8))
+        for lo in range(512, S, 256):
+            unit(1, 512, lo, lo + 256, 128)
         unit(2, 512, 512, 768, 128)
         unit(2, 768, 768, 896, 48)
         add_bias((4, 5))

@@ -27,7 +27,7 @@ def tile_list_tabx_tm_bias_kernel(tc, tab, w4_words, w4_scales, x, u, b, offs, o
     nc = tc.nc
     with ExitStack() as ctx:
         keep = ctx.enter_context(tc.tile_pool(name="keep", bufs=1))
-        psum = ctx.enter_context(tc.psum_pool(name="psum", bufs=8))
+        psum = ctx.enter_context(tc.psum_pool(name="psum", bufs=2))
 
         def held(shape, dtype, name):
             return keep.tile(shape, dtype, name=name, align_bytes=64)
@@ -41,7 +41,9 @@ def tile_list_tabx_tm_bias_kernel(tc, tab, w4_words, w4_scales, x, u, b, offs, o
         u_raw = {}
         x_raw = {}
 
-        stage = [held([P, 4 * S], F32, "stage%d" % n) for n in range(3)]
+        one = held([P, 4608], F32, "arena_one")
+        two = held([P, 4608], F32, "arena_two")
+        fresh = held([P, 4352], F32, "fresh_rooms")
 
         def load_u(room):
             rows = u.rearrange("(g p i) n -> p g (i n)", p=P, i=PACK)
@@ -96,18 +98,20 @@ def tile_list_tabx_tm_bias_kernel(tc, tab, w4_words, w4_scales, x, u, b, offs, o
 
         x_codes = [held([P, S], U32, "x_codes%d" % g) for g in range(PASSES)]
         x_plane = [held([P, S], U8, "x_plane%d" % g) for g in range(PASSES)]
-        x_grouped = [held([P, S, PACK], BF16, "x_grouped%d" % g) for g in range(PASSES)]
+        x_grouped = {}
 
-        def interleave_x(g, base, lo, hi, on_vector):
+        def interleave_x(g, base, lo, hi, on_vector, words):
             raw = x_raw[g, base]
-            mid = hi - on_vector
+            room = words.bitcast(BF16).rearrange("p (w t) -> p w t", t=PACK)
+            x_grouped[g, lo] = room
+            mid = lo + on_vector
             if lo < mid:
-                interleave(nc.scalar.copy, x_grouped[g][:, lo:mid, :], raw[:, :, lo - base : mid - base])
+                interleave(nc.vector.tensor_copy, room[:, 0:on_vector, :], raw[:, :, lo - base : mid - base])
             if mid < hi:
-                interleave(nc.vector.tensor_copy, x_grouped[g][:, mid:hi, :], raw[:, :, mid - base : hi - base])
+                interleave(nc.scalar.copy, room[:, on_vector : hi - lo, :], raw[:, :, mid - base : hi - base])
 
         def quantize_x(g, lo, hi):
-            quantize(x_codes[g][:, lo:hi], x_plane[g][:, lo:hi], x_grouped[g][:, lo:hi, :])
+            quantize(x_codes[g][:, lo:hi], x_plane[g][:, lo:hi], x_grouped[g, lo])
 
         bias = held([P, M], F32, "bias")
 
@@ -133,59 +137,80 @@ def tile_list_tabx_tm_bias_kernel(tc, tab, w4_words, w4_scales, x, u, b, offs, o
             picks = offsets[:, lo // 16 : hi // 16]
             nc.vector.tensor_copy(got_scales[:, lo:hi], tab_scales[:].bitcast(U8).indirect(picks))
 
-        acc = {}
+        group_of = {0: (0,), 1: (1,), 2: (2,), 3: (3,), 4: (4, 5), 5: (4, 5), 6: (6, 7), 7: (6, 7)}
+        banks = {}
+        passes_done = {}
+
+        def one_pass(t, cols, lhsT, lhsT_scale, rhs, rhs_scale):
+            group = group_of[t]
+            if group not in banks:
+                banks[group] = psum.tile([P, len(group), M], F32, name="sums%d" % (group[0] % 4), bufs=1)
+                passes_done[group] = 0
+            done = passes_done[group]
+            passes_done[group] = done + 1
+            nc.tensor.matmul_mx(
+                out=banks[group][:, t - group[0], cols],
+                lhsT=lhsT,
+                lhsT_scale=lhsT_scale,
+                rhs=rhs,
+                rhs_scale=rhs_scale,
+                start=(done == 0),
+                stop=(done == len(group) * (PASSES + 2) - 1),
+            )
 
         def table_passes(tiles):
             for t in tiles:
                 tok = slice(t * P, (t + 1) * P)
                 for h in range(2):
-                    nc.tensor.matmul_mx(
-                        out=acc[t][:, HALF * h : HALF * (h + 1)],
-                        lhsT=got_words[:, tok].bitcast(E4M3),
-                        lhsT_scale=planes[:].bitcast(U8)[:, tok],
-                        rhs=w4_codes[:, 2 * HALF * h : 2 * HALF * (h + 1)].bitcast(E2M1),
-                        rhs_scale=planes[:].bitcast(U8)[:, S + HALF * h : S + HALF * (h + 1)],
-                        start=False,
-                        stop=False,
+                    one_pass(
+                        t,
+                        slice(HALF * h, HALF * (h + 1)),
+                        got_words[:, tok].bitcast(E4M3),
+                        planes[:].bitcast(U8)[:, tok],
+                        w4_codes[:, 2 * HALF * h : 2 * HALF * (h + 1)].bitcast(E2M1),
+                        planes[:].bitcast(U8)[:, S + HALF * h : S + HALF * (h + 1)],
                     )
 
         def x_passes(g, tiles):
             for t in tiles:
-                if g == 0:
-                    acc[t] = psum.tile([P, M], F32, name="bank")
                 tok = slice(t * P, (t + 1) * P)
-                nc.tensor.matmul_mx(
-                    out=acc[t][:],
-                    lhsT=x_codes[g][:, tok].bitcast(E4M3),
-                    lhsT_scale=x_plane[g][:, tok],
-                    rhs=u_codes[g][:].bitcast(E4M3),
-                    rhs_scale=u_plane[g][:],
-                    start=(g == 0),
-                    stop=(g == PASSES - 1),
+                one_pass(
+                    t,
+                    slice(0, M),
+                    x_codes[g][:, tok].bitcast(E4M3),
+                    x_plane[g][:, tok],
+                    u_codes[g][:].bitcast(E4M3),
+                    u_plane[g][:],
                 )
 
         result = held([P, S // P, M], F32, "result")
         out_tiles = out.rearrange("(t p) n -> p t n", p=P)
 
-        def add_bias(tiles):
-            for t in tiles:
-                nc.vector.tensor_tensor(result[:, t, :], acc[t][:], bias[:], ADD)
+        middle = one[:, 2048:2560].rearrange("p (t s) -> p t s", t=2)
+
+        def result_of(lo, hi):
+            if lo in (4, 5):
+                return middle[:, lo - 4 : hi - 4, :]
+            return result[:, lo:hi, :]
+
+        def add_bias(t):
+            group = group_of[t]
+            rows = bias[:].unsqueeze(1).to_broadcast([P, len(group), M])
+            nc.vector.tensor_tensor(result_of(group[0], group[-1] + 1), banks[group][:], rows, ADD)
 
         def store(lo, hi):
-            nc.sync.dma_start(out_tiles[:, lo:hi, :], result[:, lo:hi, :])
+            nc.sync.dma_start(out_tiles[:, lo:hi, :], result_of(lo, hi))
 
         nc.gpsimd.memset(b_rows[:], 0.0)
         nc.gpsimd.memset(tab_scales[:, 0:768], 0)
         nc.vector.memset(tab_scales[:, 768:1024], 0)
         nc.vector.memset(planes[:], 0)
-        load_u(stage[0][:, 512:3584])
+        load_u(one[:, 0:3072])
         nc.sync.dma_start(offsets[:], offs)
         load_scales()
         load_small()
         load_words()
-        load_x(0, 0, 512, stage[1][:, 0:2048])
-        load_x(1, 0, 512, stage[1][:, 2048:4096])
-        load_x(2, 0, 512, stage[2][:, 0:2048])
+        load_x(0, 0, 512, two[:, 1280:3328])
 
         for lo in range(0, S, 512):
             gather_scales(lo, lo + 512)
@@ -195,38 +220,51 @@ def tile_list_tabx_tm_bias_kernel(tc, tab, w4_words, w4_scales, x, u, b, offs, o
             quantize_u(g)
         for lo in range(0, S, 512):
             gather_words(lo, lo + 512)
-        load_x(0, 512, S, stage[0][:, 0:2048])
-        load_x(1, 512, S, stage[0][:, 2048:4096])
+        load_x(1, 0, 512, one[:, 512:2560])
+        load_x(2, 0, 512, one[:, 2560:4608])
         spread_bias()
 
-        def unit(g, base, lo, hi, on_vector):
-            interleave_x(g, base, lo, hi, on_vector)
+        def finish(g, lo, hi):
             quantize_x(g, lo, hi)
             x_passes(g, range(lo // P, hi // P))
 
-        for g in range(PASSES):
-            if g == 2:
-                table_passes(range(4))
-            for lo in range(0, 512, 256):
-                unit(g, 0, lo, lo + 256, 128)
-            if g == 0:
-                load_x(2, 512, 768, stage[1][:, 0:1024])
-                load_x(2, 768, 896, stage[1][:, 1024:1536])
-                load_x(2, 896, S, stage[1][:, 1536:2048])
-        add_bias((0, 1))
-        unit(0, 512, 512, 768, 64)
-        add_bias((2, 3))
+        def two_units(g, rooms):
+            interleave_x(g, 0, 0, 256, 128, rooms[:, 0:512])
+            interleave_x(g, 0, 256, 512, 128, rooms[:, 512:1024])
+            finish(g, 0, 256)
+            finish(g, 256, 512)
+
+        two_units(0, fresh[:, 0:1024])
+        load_x(0, 512, S, two[:, 0:2048])
+        load_x(1, 512, S, two[:, 2304:4352])
+        table_passes(range(4))
+        two_units(1, fresh[:, 1024:2048])
+        load_x(2, 512, 768, one[:, 256:1280])
+        load_x(2, 768, 896, one[:, 1536:2048])
+        load_x(2, 896, S, one[:, 2048:2560])
+        two_units(2, fresh[:, 2048:3072])
+        add_bias(0)
+        table_passes((4, 5))
+        add_bias(1)
+        interleave_x(0, 512, 512, 768, 64, fresh[:, 3072:3584])
+        add_bias(2)
+        table_passes((6, 7))
+        finish(0, 512, 768)
+        add_bias(3)
         store(0, 4)
-        unit(0, 512, 768, S, 64)
-        table_passes(range(4, 8))
-        for lo in range(512, S, 256):
-            unit(1, 512, lo, lo + 256, 128)
-        unit(2, 512, 512, 768, 128)
-        unit(2, 768, 768, 896, 48)
-        add_bias((4, 5))
+        interleave_x(0, 512, 768, S, 64, fresh[:, 3584:4096])
+        finish(0, 768, S)
+        interleave_x(1, 512, 512, 768, 128, two[:, 1792:2304])
+        interleave_x(1, 512, 768, S, 128, two[:, 1280:1792])
+        finish(1, 512, 768)
+        interleave_x(2, 512, 512, 768, 128, two[:, 4096:4608])
+        finish(1, 768, S)
+        finish(2, 512, 768)
+        interleave_x(2, 768, 768, 896, 0, fresh[:, 4096:4352])
+        interleave_x(2, 896, 896, S, 64, one[:, 1152:1408])
+        finish(2, 768, 896)
+        finish(2, 896, S)
+        add_bias(4)
         store(4, 6)
-        unit(2, 896, 896, S, 64)
-        add_bias((6,))
-        store(6, 7)
-        add_bias((7,))
-        store(7, 8)
+        add_bias(6)
+        store(6, 8)

@@ -20,7 +20,15 @@ P = 128
 PACK = 4
 K_PASS = P * PACK
 PASSES = L // K_PASS
-HALF = M // 2
+N_TABLE = M // 2
+HALF = S // 2
+UNIT = 256
+ALIGN = 256
+ZEROED_BY_GPSIMD = 768
+
+EVEN_SHARE = 128
+SHARE_BESIDE_EVICTIONS = 64
+SHARE_OF_LAST_TILE = 64
 
 
 def tile_list_tabx_tm_bias_kernel(tc, tab, w4_words, w4_scales, x, u, b, offs, out):
@@ -30,7 +38,7 @@ def tile_list_tabx_tm_bias_kernel(tc, tab, w4_words, w4_scales, x, u, b, offs, o
         psum = ctx.enter_context(tc.psum_pool(name="psum", bufs=2))
 
         def held(shape, dtype, name):
-            return keep.tile(shape, dtype, name=name, align_bytes=64)
+            return keep.tile(shape, dtype, name=name, align_bytes=ALIGN)
 
         offsets = keep.tile([P, S // 16], U16, name="offsets")
         tab_words = held([P, T], I32, "tab_words")
@@ -38,26 +46,26 @@ def tile_list_tabx_tm_bias_kernel(tc, tab, w4_words, w4_scales, x, u, b, offs, o
         w4_codes = held([P, 2 * M], U8, "w4_codes")
         b_col = held([P, 2], F32, "b_col")
         b_rows = held([P, P], F32, "b_rows")
-        u_raw = {}
-        x_raw = {}
 
         one = held([P, 4608], F32, "arena_one")
         two = held([P, 4608], F32, "arena_two")
         fresh = held([P, 4352], F32, "fresh_rooms")
+        u_raw = {}
+        x_raw = {}
 
-        def load_u(room):
+        def load_u(words):
             rows = u.rearrange("(g p i) n -> p g (i n)", p=P, i=PACK)
-            nc.sync.dma_start(room.rearrange("p (g w) -> p g w", g=PASSES), rows)
+            nc.sync.dma_start(words.rearrange("p (g w) -> p g w", g=PASSES), rows)
             for g in range(PASSES):
-                u_raw[g] = room[:, g * PACK * M : (g + 1) * PACK * M].rearrange("p (i n) -> p i n", i=PACK)
+                u_raw[g] = words[:, g * PACK * M : (g + 1) * PACK * M].rearrange("p (i n) -> p i n", i=PACK)
 
-        def load_x(g, lo, hi, room):
-            raw = room.rearrange("p (i j) -> p i j", i=PACK)
+        def load_x(g, lo, hi, words):
+            raw = words.rearrange("p (i j) -> p i j", i=PACK)
             rows = x[g * K_PASS : (g + 1) * K_PASS, :].rearrange("(p i) j -> p i j", i=PACK)
             nc.sync.dma_start(raw, rows[:, :, lo:hi])
             x_raw[g, lo] = raw
 
-        def load_small():
+        def preload_b_and_w4():
             nc.sync.dma_start(b_rows[0:2, :], b.rearrange("(c n) -> c n", c=2))
             nc.sync.dma_start(w4_codes[:].bitcast(I32), w4_words[0].bitcast(I32))
 
@@ -86,32 +94,22 @@ def tile_list_tabx_tm_bias_kernel(tc, tab, w4_words, w4_scales, x, u, b, offs, o
         u_plane = [held([P, M], U8, "u_plane%d" % g) for g in range(PASSES)]
         u_grouped = [held([P, M, PACK], BF16, "u_grouped%d" % g) for g in range(PASSES)]
 
-        def interleave_u(g, on_vector=0):
-            mid = M - on_vector
-            if mid > 0:
-                interleave(nc.scalar.copy, u_grouped[g][:, 0:mid, :], u_raw[g][:, :, 0:mid])
-            if mid < M:
-                interleave(nc.vector.tensor_copy, u_grouped[g][:, mid:M, :], u_raw[g][:, :, mid:M])
-
-        def quantize_u(g):
-            quantize(u_codes[g][:], u_plane[g][:], u_grouped[g][:])
-
         x_codes = [held([P, S], U32, "x_codes%d" % g) for g in range(PASSES)]
         x_plane = [held([P, S], U8, "x_plane%d" % g) for g in range(PASSES)]
         x_grouped = {}
 
-        def interleave_x(g, base, lo, hi, on_vector, words):
+        def interleave_on_scalar(g, base, lo, hi, words):
+            room = words.bitcast(BF16).rearrange("p (w t) -> p w t", t=PACK)
+            x_grouped[g, lo] = room
+            interleave(nc.scalar.copy, room, x_raw[g, base][:, :, lo - base : hi - base])
+
+        def interleave_shared(g, base, lo, hi, on_vector, words):
             raw = x_raw[g, base]
             room = words.bitcast(BF16).rearrange("p (w t) -> p w t", t=PACK)
             x_grouped[g, lo] = room
             mid = lo + on_vector
-            if lo < mid:
-                interleave(nc.vector.tensor_copy, room[:, 0:on_vector, :], raw[:, :, lo - base : mid - base])
-            if mid < hi:
-                interleave(nc.scalar.copy, room[:, on_vector : hi - lo, :], raw[:, :, mid - base : hi - base])
-
-        def quantize_x(g, lo, hi):
-            quantize(x_codes[g][:, lo:hi], x_plane[g][:, lo:hi], x_grouped[g, lo])
+            interleave(nc.vector.tensor_copy, room[:, 0:on_vector, :], raw[:, :, lo - base : mid - base])
+            interleave(nc.scalar.copy, room[:, on_vector : hi - lo, :], raw[:, :, mid - base : hi - base])
 
         bias = held([P, M], F32, "bias")
 
@@ -137,7 +135,8 @@ def tile_list_tabx_tm_bias_kernel(tc, tab, w4_words, w4_scales, x, u, b, offs, o
             picks = offsets[:, lo // 16 : hi // 16]
             nc.vector.tensor_copy(got_scales[:, lo:hi], tab_scales[:].bitcast(U8).indirect(picks))
 
-        group_of = {0: (0,), 1: (1,), 2: (2,), 3: (3,), 4: (4, 5), 5: (4, 5), 6: (6, 7), 7: (6, 7)}
+        group_of = {t: (t,) if t < 4 else (t - t % 2, t - t % 2 + 1) for t in range(S // P)}
+        passes_of_a_tile = PASSES + M // N_TABLE
         banks = {}
         passes_done = {}
 
@@ -155,24 +154,25 @@ def tile_list_tabx_tm_bias_kernel(tc, tab, w4_words, w4_scales, x, u, b, offs, o
                 rhs=rhs,
                 rhs_scale=rhs_scale,
                 start=(done == 0),
-                stop=(done == len(group) * (PASSES + 2) - 1),
+                stop=(done == len(group) * passes_of_a_tile - 1),
             )
 
         def table_passes(tiles):
             for t in tiles:
                 tok = slice(t * P, (t + 1) * P)
-                for h in range(2):
+                for n0 in range(0, M, N_TABLE):
                     one_pass(
                         t,
-                        slice(HALF * h, HALF * (h + 1)),
+                        slice(n0, n0 + N_TABLE),
                         got_words[:, tok].bitcast(E4M3),
                         planes[:].bitcast(U8)[:, tok],
-                        w4_codes[:, 2 * HALF * h : 2 * HALF * (h + 1)].bitcast(E2M1),
-                        planes[:].bitcast(U8)[:, S + HALF * h : S + HALF * (h + 1)],
+                        w4_codes[:, 2 * n0 : 2 * (n0 + N_TABLE)].bitcast(E2M1),
+                        planes[:].bitcast(U8)[:, S + n0 : S + n0 + N_TABLE],
                     )
 
-        def x_passes(g, tiles):
-            for t in tiles:
+        def finish(g, lo, hi):
+            quantize(x_codes[g][:, lo:hi], x_plane[g][:, lo:hi], x_grouped[g, lo])
+            for t in range(lo // P, hi // P):
                 tok = slice(t * P, (t + 1) * P)
                 one_pass(
                     t,
@@ -186,11 +186,11 @@ def tile_list_tabx_tm_bias_kernel(tc, tab, w4_words, w4_scales, x, u, b, offs, o
         result = held([P, S // P, M], F32, "result")
         out_tiles = out.rearrange("(t p) n -> p t n", p=P)
 
-        middle = one[:, 2048:2560].rearrange("p (t s) -> p t s", t=2)
+        last_load = one[:, 2048:2560]
 
         def result_of(lo, hi):
-            if lo in (4, 5):
-                return middle[:, lo - 4 : hi - 4, :]
+            if lo == 4:
+                return last_load.rearrange("p (t n) -> p t n", t=2)
             return result[:, lo:hi, :]
 
         def add_bias(t):
@@ -202,68 +202,68 @@ def tile_list_tabx_tm_bias_kernel(tc, tab, w4_words, w4_scales, x, u, b, offs, o
             nc.sync.dma_start(out_tiles[:, lo:hi, :], result_of(lo, hi))
 
         nc.gpsimd.memset(b_rows[:], 0.0)
-        nc.gpsimd.memset(tab_scales[:, 0:768], 0)
-        nc.vector.memset(tab_scales[:, 768:1024], 0)
+        nc.gpsimd.memset(tab_scales[:, 0:ZEROED_BY_GPSIMD], 0)
+        nc.vector.memset(tab_scales[:, ZEROED_BY_GPSIMD:], 0)
         nc.vector.memset(planes[:], 0)
         load_u(one[:, 0:3072])
         nc.sync.dma_start(offsets[:], offs)
         load_scales()
-        load_small()
+        preload_b_and_w4()
         load_words()
-        load_x(0, 0, 512, two[:, 1280:3328])
+        load_x(0, 0, HALF, two[:, 1280:3328])
 
-        for lo in range(0, S, 512):
-            gather_scales(lo, lo + 512)
+        for lo in range(0, S, HALF):
+            gather_scales(lo, lo + HALF)
         move_scales()
         for g in range(PASSES):
-            interleave_u(g, 0)
-            quantize_u(g)
-        for lo in range(0, S, 512):
-            gather_words(lo, lo + 512)
-        load_x(1, 0, 512, one[:, 512:2560])
-        load_x(2, 0, 512, one[:, 2560:4608])
+            interleave(nc.scalar.copy, u_grouped[g][:], u_raw[g])
+            quantize(u_codes[g][:], u_plane[g][:], u_grouped[g][:])
+        for lo in range(0, S, HALF):
+            gather_words(lo, lo + HALF)
+        load_x(1, 0, HALF, one[:, 512:2560])
+        load_x(2, 0, HALF, one[:, 2560:4608])
         spread_bias()
 
-        def finish(g, lo, hi):
-            quantize_x(g, lo, hi)
-            x_passes(g, range(lo // P, hi // P))
+        def first_half(g):
+            rooms = fresh[:, 1024 * g : 1024 * (g + 1)]
+            interleave_shared(g, 0, 0, UNIT, EVEN_SHARE, rooms[:, 0:512])
+            interleave_shared(g, 0, UNIT, HALF, EVEN_SHARE, rooms[:, 512:1024])
+            finish(g, 0, UNIT)
+            finish(g, UNIT, HALF)
 
-        def two_units(g, rooms):
-            interleave_x(g, 0, 0, 256, 128, rooms[:, 0:512])
-            interleave_x(g, 0, 256, 512, 128, rooms[:, 512:1024])
-            finish(g, 0, 256)
-            finish(g, 256, 512)
-
-        two_units(0, fresh[:, 0:1024])
-        load_x(0, 512, S, two[:, 0:2048])
-        load_x(1, 512, S, two[:, 2304:4352])
+        tile_6, tile_7 = 6 * P, 7 * P
+        first_half(0)
+        load_x(0, HALF, S, two[:, 0:2048])
+        load_x(1, HALF, S, two[:, 2304:4352])
         table_passes(range(4))
-        two_units(1, fresh[:, 1024:2048])
-        load_x(2, 512, 768, one[:, 256:1280])
-        load_x(2, 768, 896, one[:, 1536:2048])
-        load_x(2, 896, S, one[:, 2048:2560])
-        two_units(2, fresh[:, 2048:3072])
+        first_half(1)
+        load_x(2, HALF, tile_6, one[:, 256:1280])
+        load_x(2, tile_6, tile_7, one[:, 1536:2048])
+        load_x(2, tile_7, S, last_load)
+        first_half(2)
+
         add_bias(0)
         table_passes((4, 5))
         add_bias(1)
-        interleave_x(0, 512, 512, 768, 64, fresh[:, 3072:3584])
+        interleave_shared(0, HALF, HALF, tile_6, SHARE_BESIDE_EVICTIONS, fresh[:, 3072:3584])
         add_bias(2)
         table_passes((6, 7))
-        finish(0, 512, 768)
+        finish(0, HALF, tile_6)
         add_bias(3)
         store(0, 4)
-        interleave_x(0, 512, 768, S, 64, fresh[:, 3584:4096])
-        finish(0, 768, S)
-        interleave_x(1, 512, 512, 768, 128, two[:, 1792:2304])
-        interleave_x(1, 512, 768, S, 128, two[:, 1280:1792])
-        finish(1, 512, 768)
-        interleave_x(2, 512, 512, 768, 128, two[:, 4096:4608])
-        finish(1, 768, S)
-        finish(2, 512, 768)
-        interleave_x(2, 768, 768, 896, 0, fresh[:, 4096:4352])
-        interleave_x(2, 896, 896, S, 64, one[:, 1152:1408])
-        finish(2, 768, 896)
-        finish(2, 896, S)
+        interleave_shared(0, HALF, tile_6, S, SHARE_BESIDE_EVICTIONS, fresh[:, 3584:4096])
+        finish(0, tile_6, S)
+
+        interleave_shared(1, HALF, HALF, tile_6, EVEN_SHARE, two[:, 1792:2304])
+        interleave_shared(1, HALF, tile_6, S, EVEN_SHARE, two[:, 1280:1792])
+        finish(1, HALF, tile_6)
+        interleave_shared(2, HALF, HALF, tile_6, EVEN_SHARE, two[:, 4096:4608])
+        finish(1, tile_6, S)
+        finish(2, HALF, tile_6)
+        interleave_on_scalar(2, tile_6, tile_6, tile_7, fresh[:, 4096:4352])
+        interleave_shared(2, tile_7, tile_7, S, SHARE_OF_LAST_TILE, one[:, 1152:1408])
+        finish(2, tile_6, tile_7)
+        finish(2, tile_7, S)
         add_bias(4)
         store(4, 6)
         add_bias(6)

@@ -20,7 +20,7 @@ P = 128
 PACK = 4
 K_PASS = P * PACK
 PASSES = L // K_PASS
-N_TABLE = M // 2
+N_TABLE = M
 HALF = S // 2
 UNIT = 256
 ALIGN = 256
@@ -135,7 +135,7 @@ def tile_list_tabx_tm_bias_kernel(tc, tab, w4_words, w4_scales, x, u, b, offs, o
             picks = offsets[:, lo // 16 : hi // 16]
             nc.vector.tensor_copy(got_scales[:, lo:hi], tab_scales[:].bitcast(U8).indirect(picks))
 
-        group_of = {t: (t,) if t < 4 else (t - t % 2, t - t % 2 + 1) for t in range(S // P)}
+        group_of = {t: (4, 5) if t in (4, 5) else (t,) for t in range(S // P)}
         passes_of_a_tile = PASSES + M // N_TABLE
         banks = {}
         passes_done = {}
@@ -243,16 +243,16 @@ def tile_list_tabx_tm_bias_kernel(tc, tab, w4_words, w4_scales, x, u, b, offs, o
         first_half(2)
 
         add_bias(0)
-        table_passes((4, 5))
         add_bias(1)
         interleave_shared(0, HALF, HALF, tile_6, SHARE_BESIDE_EVICTIONS, fresh[:, 3072:3584])
         add_bias(2)
-        table_passes((6, 7))
         finish(0, HALF, tile_6)
+        table_passes((4, 5))
         add_bias(3)
         store(0, 4)
         interleave_shared(0, HALF, tile_6, S, SHARE_BESIDE_EVICTIONS, fresh[:, 3584:4096])
         finish(0, tile_6, S)
+        table_passes((6, 7))
 
         interleave_shared(1, HALF, HALF, tile_6, EVEN_SHARE, two[:, 1792:2304])
         interleave_shared(1, HALF, tile_6, S, EVEN_SHARE, two[:, 1280:1792])
@@ -266,5 +266,6 @@ def tile_list_tabx_tm_bias_kernel(tc, tab, w4_words, w4_scales, x, u, b, offs, o
         finish(2, tile_7, S)
         add_bias(4)
         store(4, 6)
-        add_bias(6)
-        store(6, 8)
+        for t in (6, 7):
+            add_bias(t)
+            store(t, t + 1)

@@ -135,7 +135,7 @@ def tile_list_tabx_tm_bias_kernel(tc, tab, w4_words, w4_scales, x, u, b, offs, o
             picks = offsets[:, lo // 16 : hi // 16]
             nc.vector.tensor_copy(got_scales[:, lo:hi], tab_scales[:].bitcast(U8).indirect(picks))
 
-        group_of = {t: (4, 5) if t in (4, 5) else (t,) for t in range(S // P)}
+        group_of = {t: (t,) for t in range(S // P)}
         passes_of_a_tile = PASSES + M // N_TABLE
         banks = {}
         passes_done = {}
@@ -189,8 +189,8 @@ def tile_list_tabx_tm_bias_kernel(tc, tab, w4_words, w4_scales, x, u, b, offs, o
         last_load = one[:, 2048:2560]
 
         def result_of(lo, hi):
-            if lo == 4:
-                return last_load.rearrange("p (t n) -> p t n", t=2)
+            if lo in (4, 5):
+                return last_load.rearrange("p (t n) -> p t n", t=2)[:, lo - 4 : hi - 4, :]
             return result[:, lo:hi, :]
 
         def add_bias(t):
@@ -264,8 +264,6 @@ def tile_list_tabx_tm_bias_kernel(tc, tab, w4_words, w4_scales, x, u, b, offs, o
         interleave_shared(2, tile_7, tile_7, S, SHARE_OF_LAST_TILE, one[:, 1152:1408])
         finish(2, tile_6, tile_7)
         finish(2, tile_7, S)
-        add_bias(4)
-        store(4, 6)
-        for t in (6, 7):
+        for t in range(4, 8):
             add_bias(t)
             store(t, t + 1)

@@ -66,8 +66,8 @@ def tile_list_tabx_tm_bias_kernel(tc, tab, w4_words, w4_scales, x, u, b, offs, o
             x_raw[g, lo] = raw
 
         def preload_b_and_w4():
-            nc.sync.dma_start(b_rows[0:2, :], b.rearrange("(c n) -> c n", c=2))
-            nc.sync.dma_start(w4_codes[:].bitcast(I32), w4_words[0].bitcast(I32))
+            nc.scalar.dma_start(b_rows[0:2, :], b.rearrange("(c n) -> c n", c=2))
+            nc.scalar.dma_start(w4_codes[:].bitcast(I32), w4_words[0].bitcast(I32))
 
         def load_words():
             nc.sync.dma_start(tab_words[:], tab[0, 0 : 4 * P * T].rearrange("(p w) -> p w", p=P).bitcast(I32))
@@ -77,7 +77,7 @@ def tile_list_tabx_tm_bias_kernel(tc, tab, w4_words, w4_scales, x, u, b, offs, o
 
         def load_scales():
             nc.sync.dma_start(tab_scales[4:P:8, :], tab[0, 4 * P * T :].rearrange("(q t) -> q t", q=16).bitcast(I32))
-            nc.sync.dma_start(staged[4:P:8, S // 4 :], w4_scales[0].bitcast(I32))
+            nc.scalar.dma_start(staged[4:P:8, S // 4 :], w4_scales[0].bitcast(I32))
 
         def move_scales():
             nc.vector.tensor_copy(staged[:, 0 : S // 4], got_scales[:].bitcast(I32))

@@ -24,7 +24,6 @@ N_TABLE = M
 HALF = S // 2
 UNIT = 256
 ALIGN = 256
-ZEROED_BY_GPSIMD = 768
 
 EVEN_SHARE = 128
 SHARE_BESIDE_EVICTIONS = 64
@@ -127,15 +126,13 @@ def tile_list_tabx_tm_bias_kernel(tc, tab, w4_words, w4_scales, x, u, b, offs, o
         got_words = held([P, S], U32, "got_words")
         got_scales = held([P, S], U8, "got_scales")
 
-        def gather_words(lo, hi):
-            picks = offsets[:, lo // 16 : hi // 16]
-            nc.vector.tensor_copy(got_words[:, lo:hi], tab_words[:].bitcast(U32).indirect(picks))
+        def gather_words():
+            nc.vector.tensor_copy(got_words[:], tab_words[:].bitcast(U32).indirect(offsets[:]))
 
-        def gather_scales(lo, hi):
-            picks = offsets[:, lo // 16 : hi // 16]
-            nc.vector.tensor_copy(got_scales[:, lo:hi], tab_scales[:].bitcast(U8).indirect(picks))
+        def gather_scales():
+            nc.vector.tensor_copy(got_scales[:], tab_scales[:].bitcast(U8).indirect(offsets[:]))
 
-        group_of = {t: (t,) for t in range(S // P)}
+        group_of = {t: (t - t % 2, t - t % 2 + 1) if t < 4 else (t,) for t in range(S // P)}
         passes_of_a_tile = PASSES + M // N_TABLE
         banks = {}
         passes_done = {}
@@ -202,9 +199,8 @@ def tile_list_tabx_tm_bias_kernel(tc, tab, w4_words, w4_scales, x, u, b, offs, o
             nc.sync.dma_start(out_tiles[:, lo:hi, :], result_of(lo, hi))
 
         nc.gpsimd.memset(b_rows[:], 0.0)
-        nc.gpsimd.memset(tab_scales[:, 0:ZEROED_BY_GPSIMD], 0)
-        nc.vector.memset(tab_scales[:, ZEROED_BY_GPSIMD:], 0)
-        nc.vector.memset(planes[:], 0)
+        nc.gpsimd.memset(tab_scales[:], 0)
+        nc.gpsimd.memset(planes[:], 0)
         load_u(one[:, 0:3072])
         nc.sync.dma_start(offsets[:], offs)
         load_scales()
@@ -212,24 +208,26 @@ def tile_list_tabx_tm_bias_kernel(tc, tab, w4_words, w4_scales, x, u, b, offs, o
         load_words()
         load_x(0, 0, HALF, two[:, 1280:3328])
 
-        for lo in range(0, S, HALF):
-            gather_scales(lo, lo + HALF)
+        gather_scales()
         move_scales()
         for g in range(PASSES):
             interleave(nc.scalar.copy, u_grouped[g][:], u_raw[g])
             quantize(u_codes[g][:], u_plane[g][:], u_grouped[g][:])
-        for lo in range(0, S, HALF):
-            gather_words(lo, lo + HALF)
+        gather_words()
         load_x(1, 0, HALF, one[:, 512:2560])
         load_x(2, 0, HALF, one[:, 2560:4608])
         spread_bias()
 
         def first_half(g):
             rooms = fresh[:, 1024 * g : 1024 * (g + 1)]
-            interleave_shared(g, 0, 0, UNIT, EVEN_SHARE, rooms[:, 0:512])
-            interleave_shared(g, 0, UNIT, HALF, EVEN_SHARE, rooms[:, 512:1024])
-            finish(g, 0, UNIT)
-            finish(g, UNIT, HALF)
+            interleave_shared(g, 0, 0, HALF, UNIT, rooms)
+            if g < PASSES - 1:
+                finish(g, 0, HALF)
+            else:
+                whole = x_grouped[g, 0]
+                x_grouped[g, 0], x_grouped[g, UNIT] = whole[:, 0:UNIT, :], whole[:, UNIT:HALF, :]
+                finish(g, 0, UNIT)
+                finish(g, UNIT, HALF)
 
         tile_6, tile_7 = 6 * P, 7 * P
         first_half(0)
@@ -243,12 +241,10 @@ def tile_list_tabx_tm_bias_kernel(tc, tab, w4_words, w4_scales, x, u, b, offs, o
         first_half(2)
 
         add_bias(0)
-        add_bias(1)
         interleave_shared(0, HALF, HALF, tile_6, SHARE_BESIDE_EVICTIONS, fresh[:, 3072:3584])
         add_bias(2)
         finish(0, HALF, tile_6)
         table_passes((4, 5))
-        add_bias(3)
         store(0, 4)
         interleave_shared(0, HALF, tile_6, S, SHARE_BESIDE_EVICTIONS, fresh[:, 3584:4096])
         finish(0, tile_6, S)

@@ -20,21 +20,14 @@ P = 128
 PACK = 4
 K_PASS = P * PACK
 PASSES = L // K_PASS
-N_TABLE = M
-HALF = S // 2
-UNIT = 256
 ALIGN = 256
-
-EVEN_SHARE = 128
-SHARE_BESIDE_EVICTIONS = 64
-SHARE_OF_LAST_TILE = 64
 
 
 def tile_list_tabx_tm_bias_kernel(tc, tab, w4_words, w4_scales, x, u, b, offs, out):
     nc = tc.nc
     with ExitStack() as ctx:
         keep = ctx.enter_context(tc.tile_pool(name="keep", bufs=1))
-        psum = ctx.enter_context(tc.psum_pool(name="psum", bufs=2))
+        psum = ctx.enter_context(tc.psum_pool(name="psum", bufs=1))
 
         def held(shape, dtype, name):
             return keep.tile(shape, dtype, name=name, align_bytes=ALIGN)
@@ -45,221 +38,176 @@ def tile_list_tabx_tm_bias_kernel(tc, tab, w4_words, w4_scales, x, u, b, offs, o
         w4_codes = held([P, 2 * M], U8, "w4_codes")
         b_col = held([P, 2], F32, "b_col")
         b_rows = held([P, P], F32, "b_rows")
-
-        one = held([P, 4608], F32, "arena_one")
-        two = held([P, 4608], F32, "arena_two")
-        fresh = held([P, 4352], F32, "fresh_rooms")
-        u_raw = {}
-        x_raw = {}
-
-        def load_u(words):
-            rows = u.rearrange("(g p i) n -> p g (i n)", p=P, i=PACK)
-            nc.sync.dma_start(words.rearrange("p (g w) -> p g w", g=PASSES), rows)
-            for g in range(PASSES):
-                u_raw[g] = words[:, g * PACK * M : (g + 1) * PACK * M].rearrange("p (i n) -> p i n", i=PACK)
-
-        def load_x(g, lo, hi, words):
-            raw = words.rearrange("p (i j) -> p i j", i=PACK)
-            rows = x[g * K_PASS : (g + 1) * K_PASS, :].rearrange("(p i) j -> p i j", i=PACK)
-            nc.sync.dma_start(raw, rows[:, :, lo:hi])
-            x_raw[g, lo] = raw
-
-        def preload_b_and_w4():
-            nc.scalar.dma_start(b_rows[0:2, :], b.rearrange("(c n) -> c n", c=2))
-            nc.scalar.dma_start(w4_codes[:].bitcast(I32), w4_words[0].bitcast(I32))
-
-        def load_words():
-            nc.sync.dma_start(tab_words[:], tab[0, 0 : 4 * P * T].rearrange("(p w) -> p w", p=P).bitcast(I32))
-
         staged = held([P, (S + M) // 4], I32, "staged")
         planes = held([P, (S + M) // 4], I32, "planes")
+        got_words = held([P, S], U32, "got_words")
+        got_scales = held([P, S], U8, "got_scales")
+        u_raw = held([P, PASSES, PACK * M], F32, "u_raw")
+        bias = held([P, M], F32, "bias")
+        u_codes = [held([P, M], U32, "u_codes%d" % g) for g in range(PASSES)]
+        u_plane = [held([P, M], U8, "u_plane%d" % g) for g in range(PASSES)]
+        u_room = [held([P, M, PACK], BF16, "u_room%d" % g) for g in range(PASSES)]
+        x_codes = [held([P, S], U32, "x_codes%d" % g) for g in range(PASSES)]
+        x_plane = [held([P, S], U8, "x_plane%d" % g) for g in range(PASSES)]
+        out_tiles = out.rearrange("(t p) n -> p t n", p=P)
+        raw = {}
+        room = {}
 
-        def load_scales():
-            nc.sync.dma_start(tab_scales[4:P:8, :], tab[0, 4 * P * T :].rearrange("(q t) -> q t", q=16).bitcast(I32))
-            nc.scalar.dma_start(staged[4:P:8, S // 4 :], w4_scales[0].bitcast(I32))
+        def load_x(g, t0, t1):
+            n = (t1 - t0) * P
+            raw[g, t0] = held([P, PACK * n], F32, "raw%d_%d" % (g, t0))
+            room[g, t0] = held([P, n, PACK], BF16, "room%d_%d" % (g, t0))
+            rows = x[g * K_PASS : (g + 1) * K_PASS, :].rearrange("(p i) j -> p i j", i=PACK)
+            nc.sync.dma_start(raw[g, t0][:].rearrange("p (i j) -> p i j", i=PACK), rows[:, :, t0 * P : t1 * P])
 
-        def move_scales():
-            nc.vector.tensor_copy(staged[:, 0 : S // 4], got_scales[:].bitcast(I32))
-            for r in range(4):
-                nc.sync.dma_start(planes[r:P:32, :], staged[8 * r + 4 : P : 32, :])
+        def interleave(copy, grouped, rows):
+            copy(grouped.rearrange("p (c i) t -> p c t i", i=4), rows.rearrange("p t (c i) -> p c t i", i=4))
 
-        def interleave(copy, grouped, raw):
-            copy(grouped.rearrange("p (c i) t -> p c t i", i=4), raw.rearrange("p t (c i) -> p c t i", i=4))
+        def copy_x(copy, g, t0, lo, hi):
+            rows = raw[g, t0][:].rearrange("p (i j) -> p i j", i=PACK)
+            interleave(copy, room[g, t0][:, lo:hi, :], rows[:, :, lo:hi])
 
         def quantize(codes, plane, grouped):
             nc.vector.quantize_mx(out=codes.bitcast(E4M3), scales=plane, in_=grouped.rearrange("p w t -> p (w t)"))
 
-        u_codes = [held([P, M], U32, "u_codes%d" % g) for g in range(PASSES)]
-        u_plane = [held([P, M], U8, "u_plane%d" % g) for g in range(PASSES)]
-        u_grouped = [held([P, M, PACK], BF16, "u_grouped%d" % g) for g in range(PASSES)]
-
-        x_codes = [held([P, S], U32, "x_codes%d" % g) for g in range(PASSES)]
-        x_plane = [held([P, S], U8, "x_plane%d" % g) for g in range(PASSES)]
-        x_grouped = {}
-
-        def interleave_on_scalar(g, base, lo, hi, words):
-            room = words.bitcast(BF16).rearrange("p (w t) -> p w t", t=PACK)
-            x_grouped[g, lo] = room
-            interleave(nc.scalar.copy, room, x_raw[g, base][:, :, lo - base : hi - base])
-
-        def interleave_shared(g, base, lo, hi, on_vector, words):
-            raw = x_raw[g, base]
-            room = words.bitcast(BF16).rearrange("p (w t) -> p w t", t=PACK)
-            x_grouped[g, lo] = room
-            mid = lo + on_vector
-            interleave(nc.vector.tensor_copy, room[:, 0:on_vector, :], raw[:, :, lo - base : mid - base])
-            interleave(nc.scalar.copy, room[:, on_vector : hi - lo, :], raw[:, :, mid - base : hi - base])
-
-        bias = held([P, M], F32, "bias")
-
-        def spread_bias():
-            ident = held([P, P], F32, "ident")
-            make_identity(nc, ident[:])
-            turned = psum.tile([P, P], F32, name="bank")
-            nc.tensor.transpose(turned[:], b_rows[:], ident[:])
-            nc.scalar.copy(b_col[:], turned[:, 0:2])
-            bias_bank = psum.tile([P, 2, P], F32, name="bank")
-            for c in range(2):
-                nc.tensor.transpose(bias_bank[:, c, :], b_col[:, c : c + 1].to_broadcast([P, P]), ident[:])
-            nc.scalar.copy(bias[:], bias_bank[:].rearrange("p c n -> p (c n)"))
-
-        got_words = held([P, S], U32, "got_words")
-        got_scales = held([P, S], U8, "got_scales")
-
-        def gather_words():
-            nc.vector.tensor_copy(got_words[:], tab_words[:].bitcast(U32).indirect(offsets[:]))
-
-        def gather_scales():
-            nc.vector.tensor_copy(got_scales[:], tab_scales[:].bitcast(U8).indirect(offsets[:]))
-
-        group_of = {t: (t - t % 2, t - t % 2 + 1) if t < 4 else (t,) for t in range(S // P)}
-        passes_of_a_tile = PASSES + M // N_TABLE
+        group_of = {t: (t - t % 2, t - t % 2 + 1) if t < 4 else (t,) for t in range(8)}
+        bank_of = {0: 0, 2: 1, 4: 0, 5: 2, 6: 1, 7: 3}
         banks = {}
-        passes_done = {}
+        done = {}
 
-        def one_pass(t, cols, lhsT, lhsT_scale, rhs, rhs_scale):
+        def one_pass(t, lhsT, lhsT_scale, rhs, rhs_scale):
             group = group_of[t]
             if group not in banks:
-                banks[group] = psum.tile([P, len(group), M], F32, name="sums%d" % (group[0] % 4), bufs=1)
-                passes_done[group] = 0
-            done = passes_done[group]
-            passes_done[group] = done + 1
+                banks[group] = psum.tile([P, len(group), M], F32, name="bank%d" % bank_of[group[0]])
+                done[group] = 0
             nc.tensor.matmul_mx(
-                out=banks[group][:, t - group[0], cols],
+                out=banks[group][:, t - group[0], :],
                 lhsT=lhsT,
                 lhsT_scale=lhsT_scale,
                 rhs=rhs,
                 rhs_scale=rhs_scale,
-                start=(done == 0),
-                stop=(done == len(group) * passes_of_a_tile - 1),
+                start=(done[group] == 0),
+                stop=(done[group] == len(group) * (PASSES + 1) - 1),
             )
+            done[group] = done[group] + 1
 
         def table_passes(tiles):
             for t in tiles:
                 tok = slice(t * P, (t + 1) * P)
-                for n0 in range(0, M, N_TABLE):
-                    one_pass(
-                        t,
-                        slice(n0, n0 + N_TABLE),
-                        got_words[:, tok].bitcast(E4M3),
-                        planes[:].bitcast(U8)[:, tok],
-                        w4_codes[:, 2 * n0 : 2 * (n0 + N_TABLE)].bitcast(E2M1),
-                        planes[:].bitcast(U8)[:, S + n0 : S + n0 + N_TABLE],
-                    )
-
-        def finish(g, lo, hi):
-            quantize(x_codes[g][:, lo:hi], x_plane[g][:, lo:hi], x_grouped[g, lo])
-            for t in range(lo // P, hi // P):
-                tok = slice(t * P, (t + 1) * P)
                 one_pass(
                     t,
-                    slice(0, M),
-                    x_codes[g][:, tok].bitcast(E4M3),
-                    x_plane[g][:, tok],
-                    u_codes[g][:].bitcast(E4M3),
-                    u_plane[g][:],
+                    got_words[:, tok].bitcast(E4M3),
+                    planes[:].bitcast(U8)[:, tok],
+                    w4_codes[:].bitcast(E2M1),
+                    planes[:].bitcast(U8)[:, S : S + M],
                 )
 
-        result = held([P, S // P, M], F32, "result")
-        out_tiles = out.rearrange("(t p) n -> p t n", p=P)
+        def x_passes(g, tiles):
+            for t in tiles:
+                tok = slice(t * P, (t + 1) * P)
+                one_pass(t, x_codes[g][:, tok].bitcast(E4M3), x_plane[g][:, tok], u_codes[g][:].bitcast(E4M3), u_plane[g][:])
 
-        last_load = one[:, 2048:2560]
+        def quantize_x(g, t0, ta, tb):
+            tok = slice(ta * P, tb * P)
+            quantize(x_codes[g][:, tok], x_plane[g][:, tok], room[g, t0][:, (ta - t0) * P : (tb - t0) * P, :])
 
-        def result_of(lo, hi):
-            if lo in (4, 5):
-                return last_load.rearrange("p (t n) -> p t n", t=2)[:, lo - 4 : hi - 4, :]
-            return result[:, lo:hi, :]
-
-        def add_bias(t):
+        def evict(t, words):
             group = group_of[t]
             rows = bias[:].unsqueeze(1).to_broadcast([P, len(group), M])
-            nc.vector.tensor_tensor(result_of(group[0], group[-1] + 1), banks[group][:], rows, ADD)
+            nc.vector.tensor_tensor(words.rearrange("p (t n) -> p t n", n=M), banks[group][:], rows, ADD)
 
-        def store(lo, hi):
-            nc.sync.dma_start(out_tiles[:, lo:hi, :], result_of(lo, hi))
+        def leave(t, words):
+            group = group_of[t]
+            evict(t, words)
+            nc.sync.dma_start(out_tiles[:, group[0] : group[-1] + 1, :], words.rearrange("p (t n) -> p t n", n=M))
+
+        def spread_bias():
+            ident = held([P, P], F32, "ident")
+            make_identity(nc, ident[:])
+            turned = psum.tile([P, P], F32, name="bank6")
+            nc.tensor.transpose(turned[:], b_rows[:], ident[:])
+            nc.scalar.copy(b_col[:], turned[:, 0:2])
+            bias_bank = psum.tile([P, 2, P], F32, name="bank7")
+            for c in range(2):
+                nc.tensor.transpose(bias_bank[:, c, :], b_col[:, c : c + 1].to_broadcast([P, P]), ident[:])
+            nc.scalar.copy(bias[:], bias_bank[:].rearrange("p c n -> p (c n)"))
+
+        on_vector = nc.vector.tensor_copy
+        on_scalar = nc.scalar.copy
 
         nc.gpsimd.memset(b_rows[:], 0.0)
         nc.gpsimd.memset(tab_scales[:], 0)
         nc.gpsimd.memset(planes[:], 0)
-        load_u(one[:, 0:3072])
+        nc.sync.dma_start(u_raw[:], u.rearrange("(g p i) n -> p g (i n)", p=P, i=PACK))
         nc.sync.dma_start(offsets[:], offs)
-        load_scales()
-        preload_b_and_w4()
-        load_words()
-        load_x(0, 0, HALF, two[:, 1280:3328])
+        nc.sync.dma_start(tab_scales[4:P:8, :], tab[0, 4 * P * T :].rearrange("(q t) -> q t", q=16).bitcast(I32))
+        nc.scalar.dma_start(staged[4:P:8, S // 4 :], w4_scales[0].bitcast(I32))
+        nc.scalar.dma_start(b_rows[0:2, :], b.rearrange("(c n) -> c n", c=2))
+        nc.scalar.dma_start(w4_codes[:].bitcast(I32), w4_words[0].bitcast(I32))
+        nc.sync.dma_start(tab_words[:], tab[0, 0 : 4 * P * T].rearrange("(p w) -> p w", p=P).bitcast(I32))
+        load_x(0, 0, 4)
 
-        gather_scales()
-        move_scales()
+        nc.vector.tensor_copy(got_scales[:], tab_scales[:].bitcast(U8).indirect(offsets[:]))
+        nc.vector.tensor_copy(staged[:, 0 : S // 4], got_scales[:].bitcast(I32))
+        for r in range(4):
+            nc.sync.dma_start(planes[r:P:32, :], staged[8 * r + 4 : P : 32, :])
         for g in range(PASSES):
-            interleave(nc.scalar.copy, u_grouped[g][:], u_raw[g])
-            quantize(u_codes[g][:], u_plane[g][:], u_grouped[g][:])
-        gather_words()
-        load_x(1, 0, HALF, one[:, 512:2560])
-        load_x(2, 0, HALF, one[:, 2560:4608])
+            interleave(on_scalar, u_room[g][:], u_raw[:, g, :].rearrange("p (i n) -> p i n", i=PACK))
+            quantize(u_codes[g][:], u_plane[g][:], u_room[g][:])
+        nc.vector.tensor_copy(got_words[:], tab_words[:].bitcast(U32).indirect(offsets[:]))
         spread_bias()
+        for g, t0, t1 in ((1, 0, 4), (2, 0, 4), (0, 4, 8), (1, 4, 8), (2, 4, 6), (2, 6, 7), (2, 7, 8)):
+            load_x(g, t0, t1)
+        early = held([P, 4 * M], F32, "early")
+        last = held([P, M], F32, "last")
 
-        def first_half(g):
-            rooms = fresh[:, 1024 * g : 1024 * (g + 1)]
-            interleave_shared(g, 0, 0, HALF, UNIT, rooms)
+        for g in range(PASSES):
+            copy_x(on_vector, g, 0, 0, 256)
+            copy_x(on_scalar, g, 0, 256, 512)
             if g < PASSES - 1:
-                finish(g, 0, HALF)
-            else:
-                whole = x_grouped[g, 0]
-                x_grouped[g, 0], x_grouped[g, UNIT] = whole[:, 0:UNIT, :], whole[:, UNIT:HALF, :]
-                finish(g, 0, UNIT)
-                finish(g, UNIT, HALF)
+                quantize_x(g, 0, 0, 4)
+                x_passes(g, range(4))
+            if g == 0:
+                table_passes(range(4))
+        for t in (0, 2):
+            quantize_x(2, 0, t, t + 2)
+            x_passes(2, (t, t + 1))
 
-        tile_6, tile_7 = 6 * P, 7 * P
-        first_half(0)
-        load_x(0, HALF, S, two[:, 0:2048])
-        load_x(1, HALF, S, two[:, 2304:4352])
-        table_passes(range(4))
-        first_half(1)
-        load_x(2, HALF, tile_6, one[:, 256:1280])
-        load_x(2, tile_6, tile_7, one[:, 1536:2048])
-        load_x(2, tile_7, S, last_load)
-        first_half(2)
 
-        add_bias(0)
-        interleave_shared(0, HALF, HALF, tile_6, SHARE_BESIDE_EVICTIONS, fresh[:, 3072:3584])
-        add_bias(2)
-        finish(0, HALF, tile_6)
+        def unit(g, t0, lo, n, share):
+            if share:
+                copy_x(on_vector, g, t0, lo, lo + share)
+            copy_x(on_scalar, g, t0, lo + share, lo + n)
+
+
+        evict(0, early[:, 0:512])
+        unit(0, 4, 0, 256, 64)
+        evict(2, early[:, 512:1024])
+        quantize_x(0, 4, 4, 6)
+        x_passes(0, (4, 5))
         table_passes((4, 5))
-        store(0, 4)
-        interleave_shared(0, HALF, tile_6, S, SHARE_BESIDE_EVICTIONS, fresh[:, 3584:4096])
-        finish(0, tile_6, S)
+        nc.sync.dma_start(out_tiles[:, 0:4, :], early[:].rearrange("p (t n) -> p t n", n=M))
+        unit(0, 4, 256, 256, 64)
+        quantize_x(0, 4, 6, 8)
+        x_passes(0, (6, 7))
         table_passes((6, 7))
 
-        interleave_shared(1, HALF, HALF, tile_6, EVEN_SHARE, two[:, 1792:2304])
-        interleave_shared(1, HALF, tile_6, S, EVEN_SHARE, two[:, 1280:1792])
-        finish(1, HALF, tile_6)
-        interleave_shared(2, HALF, HALF, tile_6, EVEN_SHARE, two[:, 4096:4608])
-        finish(1, tile_6, S)
-        finish(2, HALF, tile_6)
-        interleave_on_scalar(2, tile_6, tile_6, tile_7, fresh[:, 4096:4352])
-        interleave_shared(2, tile_7, tile_7, S, SHARE_OF_LAST_TILE, one[:, 1152:1408])
-        finish(2, tile_6, tile_7)
-        finish(2, tile_7, S)
-        for t in range(4, 8):
-            add_bias(t)
-            store(t, t + 1)
+        unit(1, 4, 0, 256, 128)
+        unit(1, 4, 256, 256, 128)
+        quantize_x(1, 4, 4, 6)
+        x_passes(1, (4, 5))
+        unit(2, 4, 0, 256, 128)
+        quantize_x(1, 4, 6, 8)
+        x_passes(1, (6, 7))
+        quantize_x(2, 4, 4, 6)
+        x_passes(2, (4, 5))
+        unit(2, 6, 0, 128, 0)
+        unit(2, 7, 0, 128, 64)
+        quantize_x(2, 6, 6, 7)
+        x_passes(2, (6,))
+        quantize_x(2, 7, 7, 8)
+        x_passes(2, (7,))
+        leave(4, raw[2, 7][:, 0:256])
+        leave(5, raw[2, 7][:, 256:512])
+        leave(6, raw[2, 6][:, 0:256])
+        leave(7, last[:])

@@ -38,7 +38,6 @@ def tile_list_tabx_tm_bias_kernel(tc, tab, w4_words, w4_scales, x, u, b, offs, o
         w4_codes = held([P, 2 * M], U8, "w4_codes")
         b_col = held([P, 2], F32, "b_col")
         b_rows = held([P, P], F32, "b_rows")
-        staged = held([P, (S + M) // 4], I32, "staged")
         planes = held([P, (S + M) // 4], I32, "planes")
         got_words = held([P, S], U32, "got_words")
         got_scales = held([P, S], U8, "got_scales")
@@ -136,21 +135,21 @@ def tile_list_tabx_tm_bias_kernel(tc, tab, w4_words, w4_scales, x, u, b, offs, o
         on_scalar = nc.scalar.copy
 
         nc.gpsimd.memset(b_rows[:], 0.0)
+        nc.gpsimd.memset(planes[:, S // 4 :], 0)
         nc.gpsimd.memset(tab_scales[:], 0)
-        nc.gpsimd.memset(planes[:], 0)
         nc.sync.dma_start(u_raw[:], u.rearrange("(g p i) n -> p g (i n)", p=P, i=PACK))
         nc.sync.dma_start(offsets[:], offs)
-        nc.sync.dma_start(tab_scales[4:P:8, :], tab[0, 4 * P * T :].rearrange("(q t) -> q t", q=16).bitcast(I32))
-        nc.scalar.dma_start(staged[4:P:8, S // 4 :], w4_scales[0].bitcast(I32))
+        nc.sync.dma_start(tab_scales[0:P:8, :], tab[0, 4 * P * T :].rearrange("(q t) -> q t", q=16).bitcast(I32))
+        nc.scalar.dma_start(planes[0:P:8, S // 4 :], w4_scales[0].bitcast(I32))
         nc.scalar.dma_start(b_rows[0:2, :], b.rearrange("(c n) -> c n", c=2))
         nc.scalar.dma_start(w4_codes[:].bitcast(I32), w4_words[0].bitcast(I32))
         nc.sync.dma_start(tab_words[:], tab[0, 0 : 4 * P * T].rearrange("(p w) -> p w", p=P).bitcast(I32))
         load_x(0, 0, 4)
 
         nc.vector.tensor_copy(got_scales[:], tab_scales[:].bitcast(U8).indirect(offsets[:]))
-        nc.vector.tensor_copy(staged[:, 0 : S // 4], got_scales[:].bitcast(I32))
-        for r in range(4):
-            nc.sync.dma_start(planes[r:P:32, :], staged[8 * r + 4 : P : 32, :])
+        nc.vector.tensor_copy(planes[:, 0 : S // 4], got_scales[:].bitcast(I32))
+        for r in range(1, 4):
+            nc.sync.dma_start(planes[r:P:32, :], planes[8 * r : P : 32, :])
         for g in range(PASSES):
             interleave(on_scalar, u_room[g][:], u_raw[:, g, :].rearrange("p (i n) -> p i n", i=PACK))
             quantize(u_codes[g][:], u_plane[g][:], u_room[g][:])
@@ -186,7 +185,8 @@ def tile_list_tabx_tm_bias_kernel(tc, tab, w4_words, w4_scales, x, u, b, offs, o
         quantize_x(0, 4, 4, 6)
         x_passes(0, (4, 5))
         table_passes((4, 5))
-        nc.sync.dma_start(out_tiles[:, 0:4, :], early[:].rearrange("p (t n) -> p t n", n=M))
+        for t in (0, 2):
+            nc.sync.dma_start(out_tiles[:, t : t + 2, :], early[:, t * M : (t + 2) * M].rearrange("p (t n) -> p t n", n=M))
         unit(0, 4, 256, 256, 64)
         quantize_x(0, 4, 6, 8)
         x_passes(0, (6, 7))

@@ -70,7 +70,7 @@ def tile_list_tabx_tm_bias_kernel(tc, tab, w4_words, w4_scales, x, u, b, offs, o
             nc.vector.quantize_mx(out=codes.bitcast(E4M3), scales=plane, in_=grouped.rearrange("p w t -> p (w t)"))
 
         group_of = {t: (t - t % 2, t - t % 2 + 1) if t < 4 else (t,) for t in range(8)}
-        bank_of = {0: 0, 2: 1, 4: 0, 5: 2, 6: 1, 7: 3}
+        bank_of = {0: 0, 2: 1, 4: 2, 5: 3, 6: 4, 7: 5}
         banks = {}
         done = {}
 
@@ -167,7 +167,7 @@ def tile_list_tabx_tm_bias_kernel(tc, tab, w4_words, w4_scales, x, u, b, offs, o
                 quantize_x(g, 0, 0, 4)
                 x_passes(g, range(4))
             if g == 0:
-                table_passes(range(4))
+                table_passes(range(8))
         for t in (0, 2):
             quantize_x(2, 0, t, t + 2)
             x_passes(2, (t, t + 1))
@@ -184,13 +184,11 @@ def tile_list_tabx_tm_bias_kernel(tc, tab, w4_words, w4_scales, x, u, b, offs, o
         evict(2, early[:, 512:1024])
         quantize_x(0, 4, 4, 6)
         x_passes(0, (4, 5))
-        table_passes((4, 5))
         for t in (0, 2):
             nc.sync.dma_start(out_tiles[:, t : t + 2, :], early[:, t * M : (t + 2) * M].rearrange("p (t n) -> p t n", n=M))
         unit(0, 4, 256, 256, 64)
         quantize_x(0, 4, 6, 8)
         x_passes(0, (6, 7))
-        table_passes((6, 7))
 
         unit(1, 4, 0, 256, 128)
         unit(1, 4, 256, 256, 128)

@@ -190,20 +190,22 @@ def tile_list_tabx_tm_bias_kernel(tc, tab, w4_words, w4_scales, x, u, b, offs, o
         quantize_x(0, 4, 6, 8)
         x_passes(0, (6, 7))
 
-        unit(1, 4, 0, 256, 128)
-        unit(1, 4, 256, 256, 128)
+        unit(1, 4, 0, 512, 256)
         quantize_x(1, 4, 4, 6)
         x_passes(1, (4, 5))
         unit(2, 4, 0, 256, 128)
         quantize_x(1, 4, 6, 8)
         x_passes(1, (6, 7))
-        quantize_x(2, 4, 4, 6)
-        x_passes(2, (4, 5))
+        for t in (4, 5):
+            quantize_x(2, 4, t, t + 1)
+            x_passes(2, (t,))
         unit(2, 6, 0, 128, 0)
         unit(2, 7, 0, 128, 64)
         quantize_x(2, 6, 6, 7)
         x_passes(2, (6,))
-        quantize_x(2, 7, 7, 8)
+        for lo in (0, 64):
+            tok = slice(7 * P + lo, 7 * P + lo + 64)
+            quantize(x_codes[2][:, tok], x_plane[2][:, tok], room[2, 7][:, lo : lo + 64, :])
         x_passes(2, (7,))
         leave(4, raw[2, 7][:, 0:256])
         leave(5, raw[2, 7][:, 256:512])

from contextlib import ExitStack

import concourse.mybir as mybir
from concourse.masks import make_identity

K, L, M, T, S = 512, 1536, 256, 4096, 1024
FLOPS = 2 * S * M * (K + L)

F32 = mybir.dt.float32
BF16 = mybir.dt.bfloat16
I32 = mybir.dt.int32
U32 = mybir.dt.uint32
U16 = mybir.dt.uint16
U8 = mybir.dt.uint8
E4M3 = mybir.dt.float8_e4m3fn_x4
E2M1 = mybir.dt.float4_e2m1fn_x4
ADD = mybir.AluOpType.add

P = 128
PACK = 4
K_PASS = P * PACK
PASSES = L // K_PASS
ALIGN = 256


def tile_list_tabx_tm_bias_kernel(tc, tab, w4_words, w4_scales, x, u, b, offs, out):
    nc = tc.nc
    with ExitStack() as ctx:
        keep = ctx.enter_context(tc.tile_pool(name="keep", bufs=1))
        psum = ctx.enter_context(tc.psum_pool(name="psum", bufs=1))

        def held(shape, dtype, name):
            return keep.tile(shape, dtype, name=name, align_bytes=ALIGN)

        offsets = keep.tile([P, S // 16], U16, name="offsets")
        tab_words = held([P, T], I32, "tab_words")
        tab_scales = held([P, T // 4], I32, "tab_scales")
        w4_codes = held([P, 2 * M], U8, "w4_codes")
        b_col = held([P, 2], F32, "b_col")
        b_rows = held([P, P], F32, "b_rows")
        planes = held([P, (S + M) // 4], I32, "planes")
        got_words = held([P, S], U32, "got_words")
        got_scales = held([P, S], U8, "got_scales")
        u_raw = held([P, PASSES, PACK * M], F32, "u_raw")
        bias = held([P, M], F32, "bias")
        u_codes = [held([P, M], U32, "u_codes%d" % g) for g in range(PASSES)]
        u_plane = [held([P, M], U8, "u_plane%d" % g) for g in range(PASSES)]
        u_room = [held([P, M, PACK], BF16, "u_room%d" % g) for g in range(PASSES)]
        x_codes = [held([P, S], U32, "x_codes%d" % g) for g in range(PASSES)]
        x_plane = [held([P, S], U8, "x_plane%d" % g) for g in range(PASSES)]
        out_tiles = out.rearrange("(t p) n -> p t n", p=P)
        raw = {}
        room = {}

        def load_x(g, t0, t1):
            n = (t1 - t0) * P
            raw[g, t0] = held([P, PACK * n], F32, "raw%d_%d" % (g, t0))
            room[g, t0] = held([P, n, PACK], BF16, "room%d_%d" % (g, t0))
            rows = x[g * K_PASS : (g + 1) * K_PASS, :].rearrange("(p i) j -> p i j", i=PACK)
            nc.sync.dma_start(raw[g, t0][:].rearrange("p (i j) -> p i j", i=PACK), rows[:, :, t0 * P : t1 * P])

        def interleave(copy, grouped, rows):
            copy(grouped.rearrange("p (c i) t -> p c t i", i=4), rows.rearrange("p t (c i) -> p c t i", i=4))

        def copy_x(copy, g, t0, lo, hi):
            rows = raw[g, t0][:].rearrange("p (i j) -> p i j", i=PACK)
            interleave(copy, room[g, t0][:, lo:hi, :], rows[:, :, lo:hi])

        def quantize(codes, plane, grouped):
            nc.vector.quantize_mx(out=codes.bitcast(E4M3), scales=plane, in_=grouped.rearrange("p w t -> p (w t)"))

        group_of = {t: (t - t % 2, t - t % 2 + 1) if t < 4 else (t,) for t in range(8)}
        bank_of = {0: 0, 2: 1, 4: 2, 5: 3, 6: 4, 7: 5}
        banks = {}
        done = {}

        def one_pass(t, lhsT, lhsT_scale, rhs, rhs_scale):
            group = group_of[t]
            if group not in banks:
                banks[group] = psum.tile([P, len(group), M], F32, name="bank%d" % bank_of[group[0]])
                done[group] = 0
            nc.tensor.matmul_mx(
                out=banks[group][:, t - group[0], :],
                lhsT=lhsT,
                lhsT_scale=lhsT_scale,
                rhs=rhs,
                rhs_scale=rhs_scale,
                start=(done[group] == 0),
                stop=(done[group] == len(group) * (PASSES + 1) - 1),
            )
            done[group] = done[group] + 1

        def table_passes(tiles):
            for t in tiles:
                tok = slice(t * P, (t + 1) * P)
                one_pass(
                    t,
                    got_words[:, tok].bitcast(E4M3),
                    planes[:].bitcast(U8)[:, tok],
                    w4_codes[:].bitcast(E2M1),
                    planes[:].bitcast(U8)[:, S : S + M],
                )

        def x_passes(g, tiles):
            for t in tiles:
                tok = slice(t * P, (t + 1) * P)
                one_pass(t, x_codes[g][:, tok].bitcast(E4M3), x_plane[g][:, tok], u_codes[g][:].bitcast(E4M3), u_plane[g][:])

        def quantize_x(g, t0, ta, tb):
            tok = slice(ta * P, tb * P)
            quantize(x_codes[g][:, tok], x_plane[g][:, tok], room[g, t0][:, (ta - t0) * P : (tb - t0) * P, :])

        def evict(t, words):
            group = group_of[t]
            rows = bias[:].unsqueeze(1).to_broadcast([P, len(group), M])
            nc.vector.tensor_tensor(words.rearrange("p (t n) -> p t n", n=M), banks[group][:], rows, ADD)

        def leave(t, words):
            group = group_of[t]
            evict(t, words)
            nc.sync.dma_start(out_tiles[:, group[0] : group[-1] + 1, :], words.rearrange("p (t n) -> p t n", n=M))

        def spread_bias():
            ident = held([P, P], F32, "ident")
            make_identity(nc, ident[:])
            turned = psum.tile([P, P], F32, name="bank6")
            nc.tensor.transpose(turned[:], b_rows[:], ident[:])
            nc.scalar.copy(b_col[:], turned[:, 0:2])
            bias_bank = psum.tile([P, 2, P], F32, name="bank7")
            for c in range(2):
                nc.tensor.transpose(bias_bank[:, c, :], b_col[:, c : c + 1].to_broadcast([P, P]), ident[:])
            nc.scalar.copy(bias[:], bias_bank[:].rearrange("p c n -> p (c n)"))

        on_vector = nc.vector.tensor_copy
        on_scalar = nc.scalar.copy

        nc.gpsimd.memset(b_rows[:], 0.0)
        nc.gpsimd.memset(planes[:, S // 4 :], 0)
        nc.gpsimd.memset(tab_scales[:], 0)
        nc.sync.dma_start(u_raw[:], u.rearrange("(g p i) n -> p g (i n)", p=P, i=PACK))
        nc.sync.dma_start(offsets[:], offs)
        nc.sync.dma_start(tab_scales[0:P:8, :], tab[0, 4 * P * T :].rearrange("(q t) -> q t", q=16).bitcast(I32))
        nc.scalar.dma_start(planes[0:P:8, S // 4 :], w4_scales[0].bitcast(I32))
        nc.scalar.dma_start(b_rows[0:2, :], b.rearrange("(c n) -> c n", c=2))
        nc.scalar.dma_start(w4_codes[:].bitcast(I32), w4_words[0].bitcast(I32))
        nc.sync.dma_start(tab_words[:], tab[0, 0 : 4 * P * T].rearrange("(p w) -> p w", p=P).bitcast(I32))
        load_x(0, 0, 4)

        nc.vector.tensor_copy(got_scales[:], tab_scales[:].bitcast(U8).indirect(offsets[:]))
        nc.vector.tensor_copy(planes[:, 0 : S // 4], got_scales[:].bitcast(I32))
        for r in range(1, 4):
            nc.sync.dma_start(planes[r:P:32, :], planes[8 * r : P : 32, :])
        for g in range(PASSES):
            interleave(on_scalar, u_room[g][:], u_raw[:, g, :].rearrange("p (i n) -> p i n", i=PACK))
            quantize(u_codes[g][:], u_plane[g][:], u_room[g][:])
        nc.vector.tensor_copy(got_words[:], tab_words[:].bitcast(U32).indirect(offsets[:]))
        spread_bias()
        for g, t0, t1 in ((1, 0, 4), (2, 0, 4), (0, 4, 8), (1, 4, 8), (2, 4, 6), (2, 6, 7), (2, 7, 8)):
            load_x(g, t0, t1)
        early = held([P, 4 * M], F32, "early")
        last = held([P, M], F32, "last")

        for g in range(PASSES):
            copy_x(on_vector, g, 0, 0, 256)
            copy_x(on_scalar, g, 0, 256, 512)
            if g < PASSES - 1:
                quantize_x(g, 0, 0, 4)
                x_passes(g, range(4))
            if g == 0:
                table_passes(range(8))
        for t in (0, 2):
            quantize_x(2, 0, t, t + 2)
            x_passes(2, (t, t + 1))


        def unit(g, t0, lo, n, share):
            if share:
                copy_x(on_vector, g, t0, lo, lo + share)
            copy_x(on_scalar, g, t0, lo + share, lo + n)


        evict(0, early[:, 0:512])
        unit(0, 4, 0, 256, 64)
        evict(2, early[:, 512:1024])
        quantize_x(0, 4, 4, 6)
        x_passes(0, (4, 5))
        for t in (0, 2):
            nc.sync.dma_start(out_tiles[:, t : t + 2, :], early[:, t * M : (t + 2) * M].rearrange("p (t n) -> p t n", n=M))
        unit(0, 4, 256, 256, 64)
        quantize_x(0, 4, 6, 8)
        x_passes(0, (6, 7))

        unit(1, 4, 0, 512, 256)
        quantize_x(1, 4, 4, 6)
        x_passes(1, (4, 5))
        unit(2, 4, 0, 256, 128)
        quantize_x(1, 4, 6, 8)
        x_passes(1, (6, 7))
        for t in (4, 5):
            quantize_x(2, 4, t, t + 1)
            x_passes(2, (t,))
        unit(2, 6, 0, 128, 0)
        unit(2, 7, 0, 128, 64)
        quantize_x(2, 6, 6, 7)
        x_passes(2, (6,))
        for lo in (0, 64):
            tok = slice(7 * P + lo, 7 * P + lo + 64)
            quantize(x_codes[2][:, tok], x_plane[2][:, tok], room[2, 7][:, lo : lo + 64, :])
        x_passes(2, (7,))
        leave(4, raw[2, 7][:, 0:256])
        leave(5, raw[2, 7][:, 256:512])
        leave(6, raw[2, 6][:, 0:256])
        leave(7, last[:])
